import numpy as np
import ml_dtypes


def mxq(x, axis, fmt="e4m3"):
    dtype, down = {"e4m3": (ml_dtypes.float8_e4m3fn, 7), "e5m2": (ml_dtypes.float8_e5m2, 14)}[fmt]
    v = np.moveaxis(np.asarray(x, np.float32).astype(ml_dtypes.bfloat16).astype(np.float64), axis, -1)
    blocks = v.reshape(v.shape[:-1] + (-1, 32))
    amax = np.abs(blocks).max(-1, keepdims=True)
    byte = np.maximum(np.where(amax > 0, np.frexp(amax)[1] - 1 + 127, 0) - down, 1)
    scale = np.exp2(byte - 127.0)
    codes = (blocks / scale).astype(np.float32).astype(dtype).astype(np.float64)
    return np.moveaxis((codes * scale).reshape(v.shape), -1, axis)


WIDE = False


def mx_kscale(k):
    if not WIDE:
        return np.ones(k)
    levels = np.array([10, -10, 5, -5, 0])
    if k % 512:
        return np.exp2(np.random.permutation(np.resize(levels, k // 32))).repeat(32)
    a = np.empty((k // 512, 16))
    for p in range(k // 512):
        a[p, :8] = np.random.permutation(np.resize(levels, 8))
        for g in range(8):
            far = levels[np.abs(levels - a[p, g]) >= 10]
            a[p, g + 8] = far[np.random.randint(len(far))]
    return np.exp2(a.ravel()).repeat(32)


def f64(x):
    return np.asarray(x).astype(np.float64)


def striped(idx):
    return np.tile(idx.reshape(-1, 16).T, (8, 1)).astype(np.uint16)


def unstriped(offs):
    return offs[:16].T.reshape(-1).astype(np.int64)


E2M1 = np.array([0.0, 0.5, 1.0, 1.5, 2.0, 3.0, 4.0, 6.0, -0.0, -0.5, -1.0, -1.5, -2.0, -3.0, -4.0, -6.0])


def pack_weight(w, fmt):
    k, n = w.shape
    w = f64(np.asarray(w, np.float32).astype(ml_dtypes.bfloat16)).reshape(k // 32, 32, n)
    amax = np.abs(w).max(1)
    if fmt == "e4m3":
        byte = np.frexp(amax)[1] - 1 + 127 - 7
    else:
        mant, ex = np.frexp(amax / 6.0)
        byte = np.where(mant > 0.5, ex, ex - 1) + 127
    byte = np.clip(np.where(amax > 0, byte, 1), 1, 254)
    scaled = (w * np.exp2(127.0 - byte)[:, None, :]).reshape(k, n).astype(np.float32)
    by_word = np.ascontiguousarray(scaled.reshape(k // 512, 128, 4, n).transpose(0, 1, 3, 2))
    if fmt == "e4m3":
        words = by_word.astype(ml_dtypes.float8_e4m3fn).view(np.uint8)
    else:
        c = by_word.astype(ml_dtypes.float4_e2m1fn).view(np.uint8) & 0xF
        words = (c[..., 0::2] | (c[..., 1::2] << 4)).reshape(k // 512, 128, 2 * n)
    return np.ascontiguousarray(words), np.ascontiguousarray(byte.astype(np.uint8).reshape(k // 512, 16, n))


def unpack_weight(words, scales, fmt):
    g, _, n = scales.shape
    words = np.ascontiguousarray(words).reshape(g, 128, n, -1)
    if fmt == "e4m3":
        vals = words.view(ml_dtypes.float8_e4m3fn).astype(np.float64)
    else:
        nib = np.empty((g, 128, n, 4), np.uint8)
        nib[..., 0::2] = words & 0xF
        nib[..., 1::2] = words >> 4
        vals = E2M1[nib]
    vals = vals * np.repeat(np.exp2(scales.astype(np.float64) - 127.0), 8, axis=1)[..., None]
    return vals.transpose(0, 1, 3, 2).reshape(g * 512, n)


def gelu(v):
    return 0.5 * v * (1.0 + np.tanh(np.sqrt(2.0 / np.pi) * (v + 0.044715 * v**3)))


K, H, N, T, S = 1024, 512, 512, 2048, 1024

def setup_inputs():
    n = np.random.standard_normal
    s = mx_kscale(K)[:, None]
    u = mx_kscale(H)[:, None]
    tab_words, tab_scales = pack_weight(n((K, T)) * s, "e4m3")
    w1_words, w1_scales = pack_weight(n((K, H)) / np.sqrt(K) / s * u.T, "e2m1")
    wr_words, wr_scales = pack_weight(n((K, N)) / np.sqrt(K) / s, "e4m3")
    return {
        "tab_words": tab_words, "tab_scales": tab_scales,
        "offs": striped(np.random.permutation(T)[:S]),
        "w1_words": w1_words, "w1_scales": w1_scales,
        "b1": (0.5 * n(H) * u[:, 0]).astype(np.float32),
        "w2": (1.2 * n((H, N)) / np.sqrt(H) / u).astype(np.float32),
        "wl": (n((K, N)) / np.sqrt(K) / s).astype(np.float32),
        "wr_words": wr_words, "wr_scales": wr_scales,
        "gr": np.exp(0.3 * n(N)).astype(np.float32),
    }

def reference(tab_words, tab_scales, offs, w1_words, w1_scales, b1, w2, wl, wr_words, wr_scales, gr):
    v = unpack_weight(tab_words, tab_scales, "e4m3")[:, unstriped(offs)]
    w1 = unpack_weight(w1_words, w1_scales, "e2m1")
    wr = unpack_weight(wr_words, wr_scales, "e4m3")
    wlq = mxq(f64(wl), 0, "e4m3")
    w2q = mxq(f64(w2), 0, "e4m3")
    h = np.maximum((w1.T @ v) + f64(b1)[:, None], 0.0)
    hq = mxq(h, 0, "e4m3")
    est = w2q.T @ hq + wlq.T @ v
    ref = f64(gr)[:, None] * (wr.T @ v)
    return np.abs(est - ref)

@@ -1,0 +1,231 @@
+from contextlib import ExitStack
+
+import concourse.mybir as mybir
+from concourse.masks import make_identity
+
+K, H, N, T, S = 1024, 512, 512, 2048, 1024
+FLOPS = 2 * S * (K * H + H * N + 2 * K * N)
+
+F32 = mybir.dt.float32
+BF16 = mybir.dt.bfloat16
+I32 = mybir.dt.int32
+U32 = mybir.dt.uint32
+U16 = mybir.dt.uint16
+U8 = mybir.dt.uint8
+FP8X4 = mybir.dt.float8_e4m3fn_x4
+FP4X4 = mybir.dt.float4_e2m1fn_x4
+ACT = mybir.ActivationFunctionType
+ALU = mybir.AluOpType
+
+P = 128
+PACK = 4
+PASSES = K // (P * PACK)
+JW = 512
+JB = S // JW
+NT = N // P
+NH = N // 2
+QUADS = 4
+
+
+def tile_list_cardinality_error_kernel(
+    tc, tab_words, tab_scales, offs, w1_words, w1_scales, b1, w2, wl, wr_words, wr_scales, gr, out
+):
+    nc = tc.nc
+    with ExitStack() as ctx:
+        keep = ctx.enter_context(tc.tile_pool(name="keep", bufs=1))
+        psum = ctx.enter_context(tc.psum_pool(name="psum", bufs=8))
+
+        def tile(shape, dtype, name):
+            return keep.tile(shape, dtype, name=name, align_bytes=64)
+
+        offsets = keep.tile([P, S // 16], U16, name="offsets")
+        stage_words = (K + H) * N // P
+        stage_early = keep.tile([P, stage_words], I32, name="stage_early", tag="stage", align_bytes=64)
+        tab_s = stage_early[:, 0 : T // 4]
+        tab_w = [tile([P, T], I32, f"tab_w{a}") for a in range(PASSES)]
+        w1_raw = tile([P, PASSES, H // 2], I32, "w1_raw")
+        w1s_raw = tile([P, PASSES, H // 4], I32, "w1s_raw")
+        w1_c = tile([P, PACK, PASSES, P // 2], I32, "w1_c")
+        w1_s = tile([P, PACK, PASSES, P // 4], I32, "w1_s")
+        wr_c = tile([P, PASSES, N], I32, "wr_c")
+        wr_s = tile([P, PASSES, N // 4], I32, "wr_s")
+        v_c = [[tile([P, JW], U32, f"v_c{a}{jb}") for jb in range(JB)] for a in range(PASSES)]
+        v_s = tile([P, S], U8, "v_s")
+        v_s1 = tile([P, S // 4], I32, "v_s1")
+        vec_rows = tile([P, P], F32, "vec_rows")
+        ident = tile([P, P], F32, "ident")
+        vec_cols = tile([P, PACK + NT], F32, "vec_cols")
+
+        nc.vector.memset(tab_s, 0)
+        nc.vector.memset(w1s_raw[:], 0)
+        nc.vector.memset(wr_s[:], 0)
+        nc.vector.memset(v_s1[:], 0)
+
+        tab_s_rows = tab_scales.bitcast(I32)
+        for q in range(QUADS):
+            nc.sync.dma_start(stage_early[32 * q : 32 * q + 8, 0 : T // 4], tab_s_rows[:, 4 * q : 4 * q + 4, :])
+        nc.sync.dma_start(offsets[:], offs)
+        tab_w_rows = tab_words.rearrange("a p t i -> a p (t i)").bitcast(I32)
+        nc.sync.dma_start(tab_w[0][:], tab_w_rows[0])
+        nc.scalar.dma_start(w1_raw[:], w1_words.bitcast(I32).rearrange("a p c -> p a c"))
+        w1s_rows = w1_scales.bitcast(I32).rearrange("a q c -> q a c")
+        for q in range(QUADS):
+            nc.scalar.dma_start(w1s_raw[32 * q : 32 * q + 4, :, :], w1s_rows[4 * q : 4 * q + 4])
+        nc.sync.dma_start(tab_w[1][:], tab_w_rows[1])
+
+        nc.gpsimd.memset(vec_rows[:], 0.0)
+        nc.gpsimd.dma_start(vec_rows[0:PACK, :], b1.rearrange("(q t i) -> t q i", t=PACK, i=8))
+        nc.gpsimd.dma_start(vec_rows[PACK : PACK + NT, :], gr.rearrange("(c p) -> c p", p=P))
+        make_identity(nc, ident[:])
+        turned = psum.tile([P, P], F32, name="turned", tag="bank")
+        nc.tensor.transpose(turned[:], vec_rows[:], ident[:])
+        nc.scalar.copy(vec_cols[:], turned[:, 0 : PACK + NT])
+
+        nc.sync.dma_start(
+            wr_c[:], wr_words.rearrange("a p c i -> a p (c i)").bitcast(I32).rearrange("a p c -> p a c")
+        )
+        wrs_rows = wr_scales.bitcast(I32).rearrange("a q c -> q a c")
+        for q in range(QUADS):
+            nc.sync.dma_start(wr_s[32 * q : 32 * q + 4, :, :], wrs_rows[4 * q : 4 * q + 4])
+
+        nc.vector.tensor_copy(v_s[:], tab_s.bitcast(U8).indirect(offsets[:]))
+        nc.scalar.dma_start(v_s1[0:112, :], v_s[4:116, :].bitcast(I32))
+
+        stage_late = keep.tile([P, stage_words], F32, name="stage_late", tag="stage", align_bytes=64)
+        chunk = PACK * NH
+        wl_raw = [
+            [
+                stage_late[:, (2 * a + hf) * chunk : (2 * a + hf + 1) * chunk].rearrange("p (i n) -> p i n", i=PACK)
+                for hf in range(2)
+            ]
+            for a in range(PASSES)
+        ]
+        w2_raw = stage_late[:, 4 * chunk : 6 * chunk].rearrange("p (t n) -> p t n", t=PACK)
+        wl_rows = wl.rearrange("(a p i) n -> a p i n", a=PASSES, i=PACK)
+        w2_rows = w2.rearrange("(q t i) n -> t q i n", t=PACK, i=8)
+        for a in range(PASSES):
+            nc.sync.dma_start(wl_raw[a][0], wl_rows[a][:, :, 0:NH])
+        for t in range(PACK):
+            nc.sync.dma_start(w2_raw[:, t, :], w2_rows[t])
+        for a in range(PASSES):
+            nc.sync.dma_start(wl_raw[a][1], wl_rows[a][:, :, NH:N])
+
+        nc.vector.tensor_copy(
+            w1_c[:].rearrange("p t a (q w) -> p t (a q) w", w=4),
+            w1_raw[:].rearrange("p a (q t w) -> p t (a q) w", t=PACK, w=4),
+        )
+        nc.vector.tensor_copy(
+            w1_s[:].rearrange("p t a (q w) -> p t (a q) w", w=2),
+            w1s_raw[:].rearrange("p a (q t w) -> p t (a q) w", t=PACK, w=2),
+        )
+        cols16 = JW // 16
+        for a in range(PASSES):
+            for jb in range(JB):
+                nc.vector.tensor_copy(
+                    v_c[a][jb][:],
+                    tab_w[a][:].bitcast(U32).indirect(offsets[:, jb * cols16 : (jb + 1) * cols16]),
+                )
+
+        def v_plane(a, jb):
+            return v_s[4 * a : P, jb * JW : (jb + 1) * JW]
+
+        def v_plane_from_zero(a, jb):
+            if a == 0:
+                return v_plane(0, jb)
+            return v_s1[:].bitcast(U8)[:, jb * JW : (jb + 1) * JW]
+
+        def interleave(dst, src):
+            nc.vector.tensor_copy(
+                dst.rearrange("p (c i t) -> p c t i", i=4, t=PACK),
+                src.rearrange("p t (c i) -> p c t i", i=4),
+            )
+
+        def quantize(src, width, name):
+            grouped = tile([P, PACK * width], BF16, name + "_g")
+            codes = tile([P, width], U32, name + "_c")
+            scales = tile([P, width], U8, name + "_s")
+            interleave(grouped[:], src)
+            nc.vector.quantize_mx(out=codes[:].bitcast(FP8X4), scales=scales[:], in_=grouped[:])
+            return codes, scales
+
+        h_rows = [tile([P, PACK, JW], BF16, f"h_rows{jb}") for jb in range(JB)]
+        for jb in range(JB):
+            for t in range(PACK):
+                acc = psum.tile([P, JW], F32, name="acc", tag="bank")
+                for a in range(PASSES):
+                    nc.tensor.matmul_mx(
+                        out=acc[:],
+                        lhsT=w1_c[:, t, a, :].bitcast(U8).bitcast(FP4X4),
+                        lhsT_scale=w1_s[:, t, a, :].bitcast(U8),
+                        rhs=v_c[a][jb][:].bitcast(FP8X4),
+                        rhs_scale=v_plane_from_zero(a, jb),
+                        start=(a == 0),
+                        stop=(a == PASSES - 1),
+                    )
+                nc.scalar.activation(h_rows[jb][:, t, :], acc[:], ACT.Relu, bias=vec_cols[:, t : t + 1])
+
+        refs = {}
+
+        def reference_tile(c, jb):
+            acc = psum.tile([P, JW], F32, name="acc", tag="bank")
+            for a in range(PASSES):
+                nc.tensor.matmul_mx(
+                    out=acc[:],
+                    lhsT=wr_c[:, a, c * P : (c + 1) * P].bitcast(FP8X4),
+                    lhsT_scale=wr_s[:, a, :].bitcast(U8)[:, c * P : (c + 1) * P],
+                    rhs=v_c[a][jb][:].bitcast(FP8X4),
+                    rhs_scale=v_plane(a, jb),
+                    start=(a == 0),
+                    stop=(a == PASSES - 1),
+                )
+            ref = tile([P, JW], F32, f"ref{c}{jb}")
+            nc.scalar.activation(ref[:], acc[:], ACT.Copy, scale=vec_cols[:, PACK + c : PACK + c + 1])
+            refs[(c, jb)] = ref
+
+        h_q = {}
+        wl_q = {}
+        w2_q = {}
+
+        def weights_half(hf):
+            for a in range(PASSES):
+                wl_q[(a, hf)] = quantize(wl_raw[a][hf], NH, f"wl{a}{hf}")
+            w2_q[hf] = quantize(w2_raw[:, :, hf * NH : (hf + 1) * NH], NH, f"w2{hf}")
+
+        def error_tile(c, jb):
+            hf, cols = c // 2, slice((c % 2) * P, (c % 2 + 1) * P)
+            acc = psum.tile([P, JW], F32, name="acc", tag="bank")
+            for a in range(PASSES):
+                codes, scales = wl_q[(a, hf)]
+                nc.tensor.matmul_mx(
+                    out=acc[:],
+                    lhsT=codes[:, cols].bitcast(FP8X4),
+                    lhsT_scale=scales[:, cols],
+                    rhs=v_c[a][jb][:].bitcast(FP8X4),
+                    rhs_scale=v_plane(a, jb),
+                    start=(a == 0),
+                    stop=False,
+                )
+            codes, scales = w2_q[hf]
+            nc.tensor.matmul_mx(
+                out=acc[:],
+                lhsT=codes[:, cols].bitcast(FP8X4),
+                lhsT_scale=scales[:, cols],
+                rhs=h_q[jb][0][:].bitcast(FP8X4),
+                rhs_scale=h_q[jb][1][:],
+                start=False,
+                stop=True,
+            )
+            diff = tile([P, JW], F32, f"diff{c}{jb}")
+            nc.vector.tensor_tensor(diff[:], acc[:], refs[(c, jb)][:], ALU.subtract)
+            err = tile([P, JW], F32, f"err{c}{jb}")
+            nc.scalar.activation(err[:], diff[:], ACT.Abs)
+            nc.sync.dma_start(out[c * P : (c + 1) * P, jb * JW : (jb + 1) * JW], err[:])
+
+        order = [(0, 0), (1, 0), (0, 1), (1, 1), (2, 0), (3, 0), (2, 1), (3, 1)]
+        h_q[0] = quantize(h_rows[0][:], JW, "h0")
+        weights_half(0)
+        h_q[1] = quantize(h_rows[1][:], JW, "h1")
+        weights_half(1)
+        for c, jb in order:
+            reference_tile(c, jb)
+            error_tile(c, jb)

@@ -25,6 +25,7 @@ JB = S // JW
 NT = N // P
 NH = N // 2
 QUADS = 4
+KIB = 1024
 
 
 def tile_list_cardinality_error_kernel(
@@ -33,91 +34,95 @@ def tile_list_cardinality_error_kernel(
     nc = tc.nc
     with ExitStack() as ctx:
         keep = ctx.enter_context(tc.tile_pool(name="keep", bufs=1))
-        psum = ctx.enter_context(tc.psum_pool(name="psum", bufs=8))
+        shared = ctx.enter_context(tc.tile_pool(name="shared", bufs=1))
+        psum = ctx.enter_context(tc.psum_pool(name="psum", bufs=1))
 
         def tile(shape, dtype, name):
             return keep.tile(shape, dtype, name=name, align_bytes=64)
 
+        def placed(shape, dtype, name, offset):
+            return shared.tile(shape, dtype, name=name, align_bytes=64, offset=offset)
+
         offsets = keep.tile([P, S // 16], U16, name="offsets")
-        stage_words = (K + H) * N // P
-        stage_early = keep.tile([P, stage_words], I32, name="stage_early", tag="stage", align_bytes=64)
-        tab_s = stage_early[:, 0 : T // 4]
-        tab_w = [tile([P, T], I32, f"tab_w{a}") for a in range(PASSES)]
-        w1_raw = tile([P, PASSES, H // 2], I32, "w1_raw")
-        w1s_raw = tile([P, PASSES, H // 4], I32, "w1s_raw")
+        tab_s = tile([P, T // 4], I32, "tab_s")
         w1_c = tile([P, PACK, PASSES, P // 2], I32, "w1_c")
         w1_s = tile([P, PACK, PASSES, P // 4], I32, "w1_s")
-        wr_c = tile([P, PASSES, N], I32, "wr_c")
-        wr_s = tile([P, PASSES, N // 4], I32, "wr_s")
         v_c = [[tile([P, JW], U32, f"v_c{a}{jb}") for jb in range(JB)] for a in range(PASSES)]
         v_s = tile([P, S], U8, "v_s")
         v_s1 = tile([P, S // 4], I32, "v_s1")
         vec_rows = tile([P, P], F32, "vec_rows")
         ident = tile([P, P], F32, "ident")
-        vec_cols = tile([P, PACK + NT], F32, "vec_cols")
+        vec_cols = tile([P, PACK], F32, "vec_cols")
 
-        nc.vector.memset(tab_s, 0)
-        nc.vector.memset(w1s_raw[:], 0)
-        nc.vector.memset(wr_s[:], 0)
-        nc.vector.memset(v_s1[:], 0)
+        zeros_first = placed([P, 9 * KIB // 4], I32, "zeros_first", 45 * KIB)
+        zeros_second = placed([P, KIB // 4], I32, "zeros_second", 55 * KIB)
+        w1s_host = placed([P, 30 * KIB // 4], I32, "w1s_host", 15 * KIB)
+        w1s_raw = w1s_host[:, 0 : PASSES * H // 4].rearrange("p (a c) -> p a c", a=PASSES)
 
-        tab_s_rows = tab_scales.bitcast(I32)
-        for q in range(QUADS):
-            nc.sync.dma_start(stage_early[32 * q : 32 * q + 8, 0 : T // 4], tab_s_rows[:, 4 * q : 4 * q + 4, :])
-        nc.sync.dma_start(offsets[:], offs)
-        tab_w_rows = tab_words.rearrange("a p t i -> a p (t i)").bitcast(I32)
-        nc.sync.dma_start(tab_w[0][:], tab_w_rows[0])
-        nc.scalar.dma_start(w1_raw[:], w1_words.bitcast(I32).rearrange("a p c -> p a c"))
-        w1s_rows = w1_scales.bitcast(I32).rearrange("a q c -> q a c")
-        for q in range(QUADS):
-            nc.scalar.dma_start(w1s_raw[32 * q : 32 * q + 4, :, :], w1s_rows[4 * q : 4 * q + 4])
-        nc.sync.dma_start(tab_w[1][:], tab_w_rows[1])
-
+        nc.vector.memset(tab_s[:], 0)
+        nc.vector.memset(zeros_first[:, 0 : S // 4], 0)
+        nc.vector.memset(zeros_second[:], 0)
+        nc.vector.tensor_copy(v_s1[:], zeros_first[:, 0 : S // 4])
+        nc.vector.tensor_copy(w1s_host[:, 0 : PASSES * H // 4], zeros_second[:])
         nc.gpsimd.memset(vec_rows[:], 0.0)
         nc.gpsimd.dma_start(vec_rows[0:PACK, :], b1.rearrange("(q t i) -> t q i", t=PACK, i=8))
-        nc.gpsimd.dma_start(vec_rows[PACK : PACK + NT, :], gr.rearrange("(c p) -> c p", p=P))
         make_identity(nc, ident[:])
-        turned = psum.tile([P, P], F32, name="turned", tag="bank")
-        nc.tensor.transpose(turned[:], vec_rows[:], ident[:])
-        nc.scalar.copy(vec_cols[:], turned[:, 0 : PACK + NT])
 
-        nc.sync.dma_start(
-            wr_c[:], wr_words.rearrange("a p c i -> a p (c i)").bitcast(I32).rearrange("a p c -> p a c")
-        )
-        wrs_rows = wr_scales.bitcast(I32).rearrange("a q c -> q a c")
+        nc.sync.dma_start(offsets[:], offs)
+        tab_s_rows = tab_scales.bitcast(I32)
         for q in range(QUADS):
-            nc.sync.dma_start(wr_s[32 * q : 32 * q + 4, :, :], wrs_rows[4 * q : 4 * q + 4])
+            nc.sync.dma_start(tab_s[32 * q : 32 * q + 8, :], tab_s_rows[:, 4 * q : 4 * q + 4, :])
+        tab_w_rows = tab_words.rearrange("a p t i -> a p (t i)").bitcast(I32)
+        tab_w = [placed([P, T], I32, f"tab_w{a}", (45 + 10 * a) * KIB) for a in range(PASSES)]
+        w1_raw = placed([P, PASSES, H // 2], I32, "w1_raw", 53 * KIB)
+        nc.sync.dma_start(tab_w[0][:], tab_w_rows[0])
+        nc.sync.dma_start(w1_raw[:], w1_words.bitcast(I32).rearrange("a p c -> p a c"))
+        w1s_rows = w1_scales.bitcast(I32).rearrange("a q c -> q a c")
+        for q in range(QUADS):
+            nc.sync.dma_start(w1s_raw[32 * q : 32 * q + 4, :, :], w1s_rows[4 * q : 4 * q + 4])
+        nc.sync.dma_start(tab_w[1][:], tab_w_rows[1])
 
-        nc.vector.tensor_copy(v_s[:], tab_s.bitcast(U8).indirect(offsets[:]))
-        nc.scalar.dma_start(v_s1[0:112, :], v_s[4:116, :].bitcast(I32))
+        banks = [psum.tile([P, JW], F32, name=f"bank{b}") for b in range(8)]
+        nc.tensor.transpose(banks[7][:, 0:P], vec_rows[:], ident[:])
+        nc.scalar.copy(vec_cols[:], banks[7][:, 0:PACK])
 
-        stage_late = keep.tile([P, stage_words], F32, name="stage_late", tag="stage", align_bytes=64)
-        chunk = PACK * NH
-        wl_raw = [
-            [
-                stage_late[:, (2 * a + hf) * chunk : (2 * a + hf + 1) * chunk].rearrange("p (i n) -> p i n", i=PACK)
-                for hf in range(2)
-            ]
-            for a in range(PASSES)
-        ]
-        w2_raw = stage_late[:, 4 * chunk : 6 * chunk].rearrange("p (t n) -> p t n", t=PACK)
-        wl_rows = wl.rearrange("(a p i) n -> a p i n", a=PASSES, i=PACK)
-        w2_rows = w2.rearrange("(q t i) n -> t q i n", t=PACK, i=8)
-        for a in range(PASSES):
-            nc.sync.dma_start(wl_raw[a][0], wl_rows[a][:, :, 0:NH])
-        for t in range(PACK):
-            nc.sync.dma_start(w2_raw[:, t, :], w2_rows[t])
-        for a in range(PASSES):
-            nc.sync.dma_start(wl_raw[a][1], wl_rows[a][:, :, NH:N])
+        nc.vector.tensor_copy(v_s[:], tab_s[:].bitcast(U8).indirect(offsets[:]))
+        nc.sync.dma_start(v_s1[0:112, :], v_s[4:116, :].bitcast(I32))
 
+        nc.vector.tensor_copy(
+            w1_s[:].rearrange("p t a (q w) -> p t (a q) w", w=2),
+            w1s_raw.rearrange("p a (q t w) -> p t (a q) w", t=PACK, w=2),
+        )
         nc.vector.tensor_copy(
             w1_c[:].rearrange("p t a (q w) -> p t (a q) w", w=4),
             w1_raw[:].rearrange("p a (q t w) -> p t (a q) w", t=PACK, w=4),
         )
-        nc.vector.tensor_copy(
-            w1_s[:].rearrange("p t a (q w) -> p t (a q) w", w=2),
-            w1s_raw[:].rearrange("p a (q t w) -> p t (a q) w", t=PACK, w=2),
+        wr_c = placed([P, PASSES, N], I32, "wr_c", 16 * KIB)
+        nc.sync.dma_start(
+            wr_c[:], wr_words.rearrange("a p c i -> a p (c i)").bitcast(I32).rearrange("a p c -> p a c")
         )
+        wr_s = placed([P, PASSES, N // 4], I32, "wr_s", 44 * KIB)
+        nc.vector.memset(wr_s[:], 0)
+        wl_raw = [
+            [placed([P, PACK, NH], F32, f"wl_raw{a}{hf}", (20 + 4 * (2 * a + hf)) * KIB) for hf in range(2)]
+            for a in range(PASSES)
+        ]
+        w2_raw = placed([P, PACK, N], F32, "w2_raw", 36 * KIB)
+        wl_rows = wl.rearrange("(a p i) n -> a p i n", a=PASSES, i=PACK)
+        w2_rows = w2.rearrange("(q t i) n -> t q i n", t=PACK, i=8)
+        wrs_rows = wr_scales.bitcast(I32).rearrange("a q c -> q a c")
+        for q in range(QUADS):
+            nc.sync.dma_start(wr_s[32 * q : 32 * q + 4, :, :], wrs_rows[4 * q : 4 * q + 4])
+        for a in range(PASSES):
+            nc.sync.dma_start(wl_raw[a][0][:], wl_rows[a][:, :, 0:NH])
+        gain = placed([P, NT], F32, "gain", 15 * KIB)
+        with nc.allow_non_contiguous_dma(reason="one factor a partition"):
+            nc.sync.dma_start(gain[:], gr.rearrange("(c p) -> p c", p=P))
+        for t in range(PACK):
+            nc.sync.dma_start(w2_raw[:, t, :], w2_rows[t])
+        for a in range(PASSES):
+            nc.sync.dma_start(wl_raw[a][1][:], wl_rows[a][:, :, NH:N])
+
         cols16 = JW // 16
         for a in range(PASSES):
             for jb in range(JB):
@@ -134,24 +139,23 @@ def tile_list_cardinality_error_kernel(
                 return v_plane(0, jb)
             return v_s1[:].bitcast(U8)[:, jb * JW : (jb + 1) * JW]
 
-        def interleave(dst, src):
-            nc.vector.tensor_copy(
+        def interleave(copy, dst, src):
+            copy(
                 dst.rearrange("p (c i t) -> p c t i", i=4, t=PACK),
                 src.rearrange("p t (c i) -> p c t i", i=4),
             )
 
-        def quantize(src, width, name):
-            grouped = tile([P, PACK * width], BF16, name + "_g")
+        def quantize(grouped, name):
+            width = grouped.shape[1] // PACK
             codes = tile([P, width], U32, name + "_c")
             scales = tile([P, width], U8, name + "_s")
-            interleave(grouped[:], src)
             nc.vector.quantize_mx(out=codes[:].bitcast(FP8X4), scales=scales[:], in_=grouped[:])
             return codes, scales
 
         h_rows = [tile([P, PACK, JW], BF16, f"h_rows{jb}") for jb in range(JB)]
         for jb in range(JB):
             for t in range(PACK):
-                acc = psum.tile([P, JW], F32, name="acc", tag="bank")
+                acc = banks[PACK * jb + t]
                 for a in range(PASSES):
                     nc.tensor.matmul_mx(
                         out=acc[:],
@@ -164,10 +168,15 @@ def tile_list_cardinality_error_kernel(
                     )
                 nc.scalar.activation(h_rows[jb][:, t, :], acc[:], ACT.Relu, bias=vec_cols[:, t : t + 1])
 
-        refs = {}
+        refs, h_q, wl_q, w2_q = {}, {}, {}, {}
+
+        def grouped(copy, src, name, kib):
+            dst = placed([P, PACK * src.shape[2]], BF16, name, (64 + kib) * KIB)
+            interleave(copy, dst[:], src)
+            return dst
 
         def reference_tile(c, jb):
-            acc = psum.tile([P, JW], F32, name="acc", tag="bank")
+            acc = banks[4 * jb + c % 2]
             for a in range(PASSES):
                 nc.tensor.matmul_mx(
                     out=acc[:],
@@ -179,23 +188,15 @@ def tile_list_cardinality_error_kernel(
                     stop=(a == PASSES - 1),
                 )
             ref = tile([P, JW], F32, f"ref{c}{jb}")
-            nc.scalar.activation(ref[:], acc[:], ACT.Copy, scale=vec_cols[:, PACK + c : PACK + c + 1])
+            nc.scalar.activation(ref[:], acc[:], ACT.Copy, scale=gain[:, c : c + 1])
             refs[(c, jb)] = ref
 
-        h_q = {}
-        wl_q = {}
-        w2_q = {}
-
-        def weights_half(hf):
-            for a in range(PASSES):
-                wl_q[(a, hf)] = quantize(wl_raw[a][hf], NH, f"wl{a}{hf}")
-            w2_q[hf] = quantize(w2_raw[:, :, hf * NH : (hf + 1) * NH], NH, f"w2{hf}")
-
         def error_tile(c, jb):
-            hf, cols = c // 2, slice((c % 2) * P, (c % 2 + 1) * P)
-            acc = psum.tile([P, JW], F32, name="acc", tag="bank")
+            hf, first = c // 2, (c % 2) * P
+            acc = banks[4 * jb + 2 + c % 2]
             for a in range(PASSES):
-                codes, scales = wl_q[(a, hf)]
+                codes, scales, base = wl_q[(a, hf)]
+                cols = slice(base + first, base + first + P)
                 nc.tensor.matmul_mx(
                     out=acc[:],
                     lhsT=codes[:, cols].bitcast(FP8X4),
@@ -208,8 +209,8 @@ def tile_list_cardinality_error_kernel(
             codes, scales = w2_q[hf]
             nc.tensor.matmul_mx(
                 out=acc[:],
-                lhsT=codes[:, cols].bitcast(FP8X4),
-                lhsT_scale=scales[:, cols],
+                lhsT=codes[:, first : first + P].bitcast(FP8X4),
+                lhsT_scale=scales[:, first : first + P],
                 rhs=h_q[jb][0][:].bitcast(FP8X4),
                 rhs_scale=h_q[jb][1][:],
                 start=False,
@@ -221,11 +222,28 @@ def tile_list_cardinality_error_kernel(
             nc.scalar.activation(err[:], diff[:], ACT.Abs)
             nc.sync.dma_start(out[c * P : (c + 1) * P, jb * JW : (jb + 1) * JW], err[:])
 
-        order = [(0, 0), (1, 0), (0, 1), (1, 1), (2, 0), (3, 0), (2, 1), (3, 1)]
-        h_q[0] = quantize(h_rows[0][:], JW, "h0")
-        weights_half(0)
-        h_q[1] = quantize(h_rows[1][:], JW, "h1")
-        weights_half(1)
-        for c, jb in order:
+        on_vector, on_scalar = nc.vector.tensor_copy, nc.scalar.copy
+        wl_first = placed([P, PASSES * PACK * NH], BF16, "wl_first", 64 * KIB)
+        for a in range(PASSES):
+            interleave(on_vector, wl_first[:, a * PACK * NH : (a + 1) * PACK * NH], wl_raw[a][0][:])
+        h_first = grouped(on_vector, h_rows[0][:], "h_first", 4)
+        codes, scales = quantize(wl_first, "wl_first")
+        for a in range(PASSES):
+            wl_q[(a, 0)] = (codes, scales, a * NH)
+        w2_first = grouped(on_vector, w2_raw[:, :, 0:NH], "w2_first", 0)
+        h_q[0] = quantize(h_first, "h_first")
+        w2_q[0] = quantize(w2_first, "w2_first")
+        for c in (0, 1):
+            reference_tile(c, 0)
+            error_tile(c, 0)
+        h_second = grouped(on_vector, h_rows[1][:], "h_second", 8)
+        w2_second = grouped(on_vector, w2_raw[:, :, NH:N], "w2_second", 4)
+        h_q[1] = quantize(h_second, "h_second")
+        w2_q[1] = quantize(w2_second, "w2_second")
+        wl_second0 = grouped(on_vector, wl_raw[0][1][:], "wl_second0", 0)
+        wl_second1 = grouped(on_scalar, wl_raw[1][1][:], "wl_second1", 8)
+        wl_q[(0, 1)] = quantize(wl_second0, "wl_second0") + (0,)
+        wl_q[(1, 1)] = quantize(wl_second1, "wl_second1") + (0,)
+        for c, jb in ((0, 1), (1, 1), (2, 0), (3, 0), (2, 1), (3, 1)):
             reference_tile(c, jb)
             error_tile(c, jb)

@@ -46,63 +46,59 @@ def tile_list_cardinality_error_kernel(
         offsets = keep.tile([P, S // 16], U16, name="offsets")
         tab_s = tile([P, T // 4], I32, "tab_s")
         w1_c = tile([P, PACK, PASSES, P // 2], I32, "w1_c")
-        w1_s = tile([P, PACK, PASSES, P // 4], I32, "w1_s")
-        v_c = [[tile([P, JW], U32, f"v_c{a}{jb}") for jb in range(JB)] for a in range(PASSES)]
+        w_s = tile([P, 2, PASSES * H // 4], I32, "w_s")
+        w1_s = w_s[:, 0, :].rearrange("p (t a m) -> p t a m", t=PACK, a=PASSES)
+        wr_s = w_s[:, 1, :].rearrange("p (a c) -> p a c", a=PASSES)
         v_s = tile([P, S], U8, "v_s")
         v_s1 = tile([P, S // 4], I32, "v_s1")
         vec_rows = tile([P, P], F32, "vec_rows")
         ident = tile([P, P], F32, "ident")
-        vec_cols = tile([P, PACK], F32, "vec_cols")
+        vec_cols = tile([P, PACK + NT], F32, "vec_cols")
 
-        zeros_first = placed([P, 9 * KIB // 4], I32, "zeros_first", 45 * KIB)
-        zeros_second = placed([P, KIB // 4], I32, "zeros_second", 55 * KIB)
-        w1s_host = placed([P, 30 * KIB // 4], I32, "w1s_host", 15 * KIB)
+        zeros_first = placed([P, KIB // 4], I32, "zeros_first", 45 * KIB)
+        zeros_second = placed([P, 2 * KIB // 4], I32, "zeros_second", 54 * KIB)
+        w1s_host = placed([P, 32 * KIB // 4], I32, "w1s_host", 13 * KIB)
         w1s_raw = w1s_host[:, 0 : PASSES * H // 4].rearrange("p (a c) -> p a c", a=PASSES)
 
         nc.vector.memset(tab_s[:], 0)
-        nc.vector.memset(zeros_first[:, 0 : S // 4], 0)
+        nc.vector.memset(vec_rows[:], 0.0)
+        nc.vector.memset(zeros_first[:], 0)
+        nc.vector.tensor_copy(v_s1[:], zeros_first[:])
         nc.vector.memset(zeros_second[:], 0)
-        nc.vector.tensor_copy(v_s1[:], zeros_first[:, 0 : S // 4])
-        nc.vector.tensor_copy(w1s_host[:, 0 : PASSES * H // 4], zeros_second[:])
-        nc.gpsimd.memset(vec_rows[:], 0.0)
-        nc.gpsimd.dma_start(vec_rows[0:PACK, :], b1.rearrange("(q t i) -> t q i", t=PACK, i=8))
+        nc.vector.tensor_copy(w1s_host[:, 0 : PASSES * H // 2], zeros_second[:])
         make_identity(nc, ident[:])
 
         nc.sync.dma_start(offsets[:], offs)
         tab_s_rows = tab_scales.bitcast(I32)
         for q in range(QUADS):
             nc.sync.dma_start(tab_s[32 * q : 32 * q + 8, :], tab_s_rows[:, 4 * q : 4 * q + 4, :])
+        nc.sync.dma_start(vec_rows[0:PACK, :], b1.rearrange("(q t i) -> t q i", t=PACK, i=8))
+        nc.sync.dma_start(vec_rows[PACK : PACK + NT, :], gr.rearrange("(c p) -> c p", p=P))
         tab_w_rows = tab_words.rearrange("a p t i -> a p (t i)").bitcast(I32)
         tab_w = [placed([P, T], I32, f"tab_w{a}", (45 + 10 * a) * KIB) for a in range(PASSES)]
         w1_raw = placed([P, PASSES, H // 2], I32, "w1_raw", 53 * KIB)
         nc.sync.dma_start(tab_w[0][:], tab_w_rows[0])
-        nc.sync.dma_start(w1_raw[:], w1_words.bitcast(I32).rearrange("a p c -> p a c"))
         w1s_rows = w1_scales.bitcast(I32).rearrange("a q c -> q a c")
         for q in range(QUADS):
             nc.sync.dma_start(w1s_raw[32 * q : 32 * q + 4, :, :], w1s_rows[4 * q : 4 * q + 4])
+        nc.sync.dma_start(w1_raw[:], w1_words.bitcast(I32).rearrange("a p c -> p a c"))
         nc.sync.dma_start(tab_w[1][:], tab_w_rows[1])
 
         banks = [psum.tile([P, JW], F32, name=f"bank{b}") for b in range(8)]
         nc.tensor.transpose(banks[7][:, 0:P], vec_rows[:], ident[:])
-        nc.scalar.copy(vec_cols[:], banks[7][:, 0:PACK])
+        nc.scalar.copy(vec_cols[:], banks[7][:, 0 : PACK + NT])
 
         nc.vector.tensor_copy(v_s[:], tab_s[:].bitcast(U8).indirect(offsets[:]))
         nc.sync.dma_start(v_s1[0:112, :], v_s[4:116, :].bitcast(I32))
 
         nc.vector.tensor_copy(
-            w1_s[:].rearrange("p t a (q w) -> p t (a q) w", w=2),
-            w1s_raw.rearrange("p a (q t w) -> p t (a q) w", t=PACK, w=2),
+            w_s[:].rearrange("p g (t b w) -> p g t b w", t=PACK, w=2),
+            w1s_host[:, 0 : PASSES * H // 2].rearrange("p (g b t w) -> p g t b w", g=2, t=PACK, w=2),
         )
         nc.vector.tensor_copy(
             w1_c[:].rearrange("p t a (q w) -> p t (a q) w", w=4),
             w1_raw[:].rearrange("p a (q t w) -> p t (a q) w", t=PACK, w=4),
         )
-        wr_c = placed([P, PASSES, N], I32, "wr_c", 16 * KIB)
-        nc.sync.dma_start(
-            wr_c[:], wr_words.rearrange("a p c i -> a p (c i)").bitcast(I32).rearrange("a p c -> p a c")
-        )
-        wr_s = placed([P, PASSES, N // 4], I32, "wr_s", 44 * KIB)
-        nc.vector.memset(wr_s[:], 0)
         wl_raw = [
             [placed([P, PACK, NH], F32, f"wl_raw{a}{hf}", (20 + 4 * (2 * a + hf)) * KIB) for hf in range(2)]
             for a in range(PASSES)
@@ -111,18 +107,23 @@ def tile_list_cardinality_error_kernel(
         wl_rows = wl.rearrange("(a p i) n -> a p i n", a=PASSES, i=PACK)
         w2_rows = w2.rearrange("(q t i) n -> t q i n", t=PACK, i=8)
         wrs_rows = wr_scales.bitcast(I32).rearrange("a q c -> q a c")
-        for q in range(QUADS):
-            nc.sync.dma_start(wr_s[32 * q : 32 * q + 4, :, :], wrs_rows[4 * q : 4 * q + 4])
         for a in range(PASSES):
             nc.sync.dma_start(wl_raw[a][0][:], wl_rows[a][:, :, 0:NH])
-        gain = placed([P, NT], F32, "gain", 15 * KIB)
-        with nc.allow_non_contiguous_dma(reason="one factor a partition"):
-            nc.sync.dma_start(gain[:], gr.rearrange("(c p) -> p c", p=P))
+        wr_c = placed([P, PASSES, N], I32, "wr_c", 16 * KIB)
+        nc.sync.dma_start(
+            wr_c[:], wr_words.rearrange("a p c i -> a p (c i)").bitcast(I32).rearrange("a p c -> p a c")
+        )
+        for q in range(QUADS):
+            nc.sync.dma_start(wr_s[32 * q : 32 * q + 4, :, :], wrs_rows[4 * q : 4 * q + 4])
         for t in range(PACK):
             nc.sync.dma_start(w2_raw[:, t, :], w2_rows[t])
         for a in range(PASSES):
             nc.sync.dma_start(wl_raw[a][1][:], wl_rows[a][:, :, NH:N])
 
+        v_c = [
+            [placed([P, JW], U32, "v_c00", 13 * KIB), placed([P, JW], U32, "v_c01", 53 * KIB)],
+            [tile([P, JW], U32, "v_c10"), tile([P, JW], U32, "v_c11")],
+        ]
         cols16 = JW // 16
         for a in range(PASSES):
             for jb in range(JB):
@@ -152,6 +153,7 @@ def tile_list_cardinality_error_kernel(
             nc.vector.quantize_mx(out=codes[:].bitcast(FP8X4), scales=scales[:], in_=grouped[:])
             return codes, scales
 
+        wl_first = placed([P, PASSES * PACK * NH], BF16, "wl_first", 64 * KIB)
         h_rows = [tile([P, PACK, JW], BF16, f"h_rows{jb}") for jb in range(JB)]
         for jb in range(JB):
             for t in range(PACK):
@@ -175,6 +177,9 @@ def tile_list_cardinality_error_kernel(
             interleave(copy, dst[:], src)
             return dst
 
+
+        ref_ring = [tile([P, JW], F32, f"ref{r}") for r in range(4)]
+
         def reference_tile(c, jb):
             acc = banks[4 * jb + c % 2]
             for a in range(PASSES):
@@ -187,8 +192,8 @@ def tile_list_cardinality_error_kernel(
                     start=(a == 0),
                     stop=(a == PASSES - 1),
                 )
-            ref = tile([P, JW], F32, f"ref{c}{jb}")
-            nc.scalar.activation(ref[:], acc[:], ACT.Copy, scale=gain[:, c : c + 1])
+            ref = ref_ring[2 * jb + c % 2][:]
+            nc.scalar.activation(ref, acc[:], ACT.Copy, scale=vec_cols[:, PACK + c : PACK + c + 1])
             refs[(c, jb)] = ref
 
         def error_tile(c, jb):
@@ -216,34 +221,43 @@ def tile_list_cardinality_error_kernel(
                 start=False,
                 stop=True,
             )
+
+        def finish_tile(c, jb):
+            acc = banks[4 * jb + 2 + c % 2]
             diff = tile([P, JW], F32, f"diff{c}{jb}")
-            nc.vector.tensor_tensor(diff[:], acc[:], refs[(c, jb)][:], ALU.subtract)
+            nc.vector.tensor_tensor(diff[:], acc[:], refs[(c, jb)], ALU.subtract)
             err = tile([P, JW], F32, f"err{c}{jb}")
             nc.scalar.activation(err[:], diff[:], ACT.Abs)
             nc.sync.dma_start(out[c * P : (c + 1) * P, jb * JW : (jb + 1) * JW], err[:])
 
         on_vector, on_scalar = nc.vector.tensor_copy, nc.scalar.copy
-        wl_first = placed([P, PASSES * PACK * NH], BF16, "wl_first", 64 * KIB)
         for a in range(PASSES):
             interleave(on_vector, wl_first[:, a * PACK * NH : (a + 1) * PACK * NH], wl_raw[a][0][:])
         h_first = grouped(on_vector, h_rows[0][:], "h_first", 4)
         codes, scales = quantize(wl_first, "wl_first")
         for a in range(PASSES):
             wl_q[(a, 0)] = (codes, scales, a * NH)
-        w2_first = grouped(on_vector, w2_raw[:, :, 0:NH], "w2_first", 0)
         h_q[0] = quantize(h_first, "h_first")
+        w2_first = grouped(on_vector, w2_raw[:, :, 0:NH], "w2_first", 0)
         w2_q[0] = quantize(w2_first, "w2_first")
         for c in (0, 1):
             reference_tile(c, 0)
             error_tile(c, 0)
         h_second = grouped(on_vector, h_rows[1][:], "h_second", 8)
-        w2_second = grouped(on_vector, w2_raw[:, :, NH:N], "w2_second", 4)
         h_q[1] = quantize(h_second, "h_second")
-        w2_q[1] = quantize(w2_second, "w2_second")
+        for c in (0, 1):
+            reference_tile(c, 1)
+            error_tile(c, 1)
+        finish_tile(0, 0)
+        w2_second = grouped(on_vector, w2_raw[:, :, NH:N], "w2_second", 4)
         wl_second0 = grouped(on_vector, wl_raw[0][1][:], "wl_second0", 0)
         wl_second1 = grouped(on_scalar, wl_raw[1][1][:], "wl_second1", 8)
+        w2_q[1] = quantize(w2_second, "w2_second")
         wl_q[(0, 1)] = quantize(wl_second0, "wl_second0") + (0,)
         wl_q[(1, 1)] = quantize(wl_second1, "wl_second1") + (0,)
-        for c, jb in ((0, 1), (1, 1), (2, 0), (3, 0), (2, 1), (3, 1)):
+        for c, jb in ((1, 0), (0, 1), (1, 1)):
+            finish_tile(c, jb)
+        for c, jb in ((2, 0), (3, 0), (2, 1), (3, 1)):
             reference_tile(c, jb)
             error_tile(c, jb)
+            finish_tile(c, jb)

@@ -154,19 +154,21 @@ def tile_list_cardinality_error_kernel(
             return codes, scales
 
         wl_first = placed([P, PASSES * PACK * NH], BF16, "wl_first", 64 * KIB)
+        interleave(nc.scalar.copy, wl_first[:, 0 : PACK * NH], wl_raw[0][0][:])
         h_rows = [tile([P, PACK, JW], BF16, f"h_rows{jb}") for jb in range(JB)]
         for jb in range(JB):
             for t in range(PACK):
                 acc = banks[PACK * jb + t]
-                for a in range(PASSES):
+                order = (0, 1) if jb == 0 else (1, 0)
+                for a in order:
                     nc.tensor.matmul_mx(
                         out=acc[:],
                         lhsT=w1_c[:, t, a, :].bitcast(U8).bitcast(FP4X4),
                         lhsT_scale=w1_s[:, t, a, :].bitcast(U8),
                         rhs=v_c[a][jb][:].bitcast(FP8X4),
                         rhs_scale=v_plane_from_zero(a, jb),
-                        start=(a == 0),
-                        stop=(a == PASSES - 1),
+                        start=(a == order[0]),
+                        stop=(a == order[-1]),
                     )
                 nc.scalar.activation(h_rows[jb][:, t, :], acc[:], ACT.Relu, bias=vec_cols[:, t : t + 1])
 
@@ -178,7 +180,8 @@ def tile_list_cardinality_error_kernel(
             return dst
 
 
-        ref_ring = [tile([P, JW], F32, f"ref{r}") for r in range(4)]
+        def estimate_bank(c, jb):
+            return banks[4 * jb + c % 2 + (2 if c < 2 else 0)]
 
         def reference_tile(c, jb):
             acc = banks[4 * jb + c % 2]
@@ -192,13 +195,13 @@ def tile_list_cardinality_error_kernel(
                     start=(a == 0),
                     stop=(a == PASSES - 1),
                 )
-            ref = ref_ring[2 * jb + c % 2][:]
+            ref = tile([P, JW], F32, f"ref{c}{jb}")[:]
             nc.scalar.activation(ref, acc[:], ACT.Copy, scale=vec_cols[:, PACK + c : PACK + c + 1])
             refs[(c, jb)] = ref
 
         def error_tile(c, jb):
             hf, first = c // 2, (c % 2) * P
-            acc = banks[4 * jb + 2 + c % 2]
+            acc = estimate_bank(c, jb)
             for a in range(PASSES):
                 codes, scales, base = wl_q[(a, hf)]
                 cols = slice(base + first, base + first + P)
@@ -222,17 +225,19 @@ def tile_list_cardinality_error_kernel(
                 stop=True,
             )
 
-        def finish_tile(c, jb):
-            acc = banks[4 * jb + 2 + c % 2]
+        def finish_tile(c, jb, pieces=1):
+            acc = estimate_bank(c, jb)
             diff = tile([P, JW], F32, f"diff{c}{jb}")
-            nc.vector.tensor_tensor(diff[:], acc[:], refs[(c, jb)], ALU.subtract)
             err = tile([P, JW], F32, f"err{c}{jb}")
-            nc.scalar.activation(err[:], diff[:], ACT.Abs)
-            nc.sync.dma_start(out[c * P : (c + 1) * P, jb * JW : (jb + 1) * JW], err[:])
+            width = JW // pieces
+            for piece in range(pieces):
+                cols = slice(piece * width, (piece + 1) * width)
+                nc.vector.tensor_tensor(diff[:, cols], acc[:, cols], refs[(c, jb)][:, cols], ALU.subtract)
+                nc.scalar.activation(err[:, cols], diff[:, cols], ACT.Abs)
+                nc.sync.dma_start(out[c * P : (c + 1) * P, jb * JW : (jb + 1) * JW][:, cols], err[:, cols])
 
         on_vector, on_scalar = nc.vector.tensor_copy, nc.scalar.copy
-        for a in range(PASSES):
-            interleave(on_vector, wl_first[:, a * PACK * NH : (a + 1) * PACK * NH], wl_raw[a][0][:])
+        interleave(on_vector, wl_first[:, PACK * NH :], wl_raw[1][0][:])
         h_first = grouped(on_vector, h_rows[0][:], "h_first", 4)
         codes, scales = quantize(wl_first, "wl_first")
         for a in range(PASSES):
@@ -248,16 +253,17 @@ def tile_list_cardinality_error_kernel(
         for c in (0, 1):
             reference_tile(c, 1)
             error_tile(c, 1)
-        finish_tile(0, 0)
-        w2_second = grouped(on_vector, w2_raw[:, :, NH:N], "w2_second", 4)
+        second_half = ((2, 0), (3, 0), (2, 1), (3, 1))
         wl_second0 = grouped(on_vector, wl_raw[0][1][:], "wl_second0", 0)
+        w2_second = grouped(on_vector, w2_raw[:, :, NH:N], "w2_second", 4)
         wl_second1 = grouped(on_scalar, wl_raw[1][1][:], "wl_second1", 8)
-        w2_q[1] = quantize(w2_second, "w2_second")
-        wl_q[(0, 1)] = quantize(wl_second0, "wl_second0") + (0,)
-        wl_q[(1, 1)] = quantize(wl_second1, "wl_second1") + (0,)
-        for c, jb in ((1, 0), (0, 1), (1, 1)):
-            finish_tile(c, jb)
-        for c, jb in ((2, 0), (3, 0), (2, 1), (3, 1)):
+        for c, jb in second_half:
             reference_tile(c, jb)
-            error_tile(c, jb)
+        wl_q[(0, 1)] = quantize(wl_second0, "wl_second0") + (0,)
+        w2_q[1] = quantize(w2_second, "w2_second")
+        wl_q[(1, 1)] = quantize(wl_second1, "wl_second1") + (0,)
+        for c, jb in ((0, 0), (1, 0), (0, 1), (1, 1)):
             finish_tile(c, jb)
+        for c, jb in second_half:
+            error_tile(c, jb)
+            finish_tile(c, jb, 2 if (c, jb) == second_half[-1] else 1)

@@ -25,7 +25,23 @@ JB = S // JW
 NT = N // P
 NH = N // 2
 QUADS = 4
+PLANE_ROWS = 4
+SHIFT_ROWS = 112
+RUN = 8
+BANKS = 8
 KIB = 1024
+
+AT_TABLE1 = 2 * KIB
+AT_ZEROS_SECOND = 9 * KIB + 512
+AT_W1 = 11 * KIB
+AT_V01 = 12 * KIB
+AT_SCALE_STAGE = 13 * KIB
+AT_WR = 16 * KIB
+AT_WL_FIRST_PASS = 20 * KIB
+AT_WL_SECOND_PASS = 28 * KIB
+AT_W2 = 36 * KIB
+AT_TABLE0 = 45 * KIB
+AT_GROUP = (64 * KIB, 68 * KIB, 72 * KIB)
 
 
 def tile_list_cardinality_error_kernel(
@@ -55,85 +71,94 @@ def tile_list_cardinality_error_kernel(
         ident = tile([P, P], F32, "ident")
         vec_cols = tile([P, PACK + NT], F32, "vec_cols")
 
-        zeros_first = placed([P, KIB // 4], I32, "zeros_first", 45 * KIB)
-        zeros_second = placed([P, 2 * KIB // 4], I32, "zeros_second", 54 * KIB)
-        w1s_host = placed([P, 32 * KIB // 4], I32, "w1s_host", 13 * KIB)
-        w1s_raw = w1s_host[:, 0 : PASSES * H // 4].rearrange("p (a c) -> p a c", a=PASSES)
+        zeros_first = placed([P, P], F32, "zeros_first", AT_TABLE0)
+        zeros_second = placed([P, 2 * KIB // 4], I32, "zeros_second", AT_ZEROS_SECOND)
+        scale_stage = placed([P, 32 * KIB // 4], I32, "scale_stage", AT_SCALE_STAGE)
+        w1s_raw = scale_stage[:, 0 : PASSES * H // 4].rearrange("p (a c) -> p a c", a=PASSES)
 
         nc.vector.memset(tab_s[:], 0)
-        nc.vector.memset(vec_rows[:], 0.0)
-        nc.vector.memset(zeros_first[:], 0)
-        nc.vector.tensor_copy(v_s1[:], zeros_first[:])
+        nc.vector.memset(zeros_first[:], 0.0)
+        nc.vector.tensor_copy(vec_rows[:], zeros_first[:])
         nc.vector.memset(zeros_second[:], 0)
-        nc.vector.tensor_copy(w1s_host[:, 0 : PASSES * H // 2], zeros_second[:])
+        nc.vector.tensor_copy(scale_stage[:, 0 : PASSES * H // 2], zeros_second[:])
+        nc.vector.memset(v_s1[:], 0)
         make_identity(nc, ident[:])
 
         nc.sync.dma_start(offsets[:], offs)
         tab_s_rows = tab_scales.bitcast(I32)
         for q in range(QUADS):
-            nc.sync.dma_start(tab_s[32 * q : 32 * q + 8, :], tab_s_rows[:, 4 * q : 4 * q + 4, :])
-        nc.sync.dma_start(vec_rows[0:PACK, :], b1.rearrange("(q t i) -> t q i", t=PACK, i=8))
+            nc.sync.dma_start(
+                tab_s[32 * q : 32 * q + PASSES * PLANE_ROWS, :],
+                tab_s_rows[:, PLANE_ROWS * q : PLANE_ROWS * (q + 1), :],
+            )
+        nc.sync.dma_start(vec_rows[0:PACK, :], b1.rearrange("(b t i) -> t b i", t=PACK, i=RUN))
         nc.sync.dma_start(vec_rows[PACK : PACK + NT, :], gr.rearrange("(c p) -> c p", p=P))
         tab_w_rows = tab_words.rearrange("a p t i -> a p (t i)").bitcast(I32)
-        tab_w = [placed([P, T], I32, f"tab_w{a}", (45 + 10 * a) * KIB) for a in range(PASSES)]
-        w1_raw = placed([P, PASSES, H // 2], I32, "w1_raw", 53 * KIB)
+        tab_w = [placed([P, T], I32, "tab_w0", AT_TABLE0), placed([P, T], I32, "tab_w1", AT_TABLE1)]
+        w1_raw = placed([P, PASSES, H // 2], I32, "w1_raw", AT_W1)
         nc.sync.dma_start(tab_w[0][:], tab_w_rows[0])
         w1s_rows = w1_scales.bitcast(I32).rearrange("a q c -> q a c")
         for q in range(QUADS):
-            nc.sync.dma_start(w1s_raw[32 * q : 32 * q + 4, :, :], w1s_rows[4 * q : 4 * q + 4])
+            nc.sync.dma_start(
+                w1s_raw[32 * q : 32 * q + PLANE_ROWS, :, :], w1s_rows[PLANE_ROWS * q : PLANE_ROWS * (q + 1)]
+            )
         nc.sync.dma_start(w1_raw[:], w1_words.bitcast(I32).rearrange("a p c -> p a c"))
         nc.sync.dma_start(tab_w[1][:], tab_w_rows[1])
 
-        banks = [psum.tile([P, JW], F32, name=f"bank{b}") for b in range(8)]
-        nc.tensor.transpose(banks[7][:, 0:P], vec_rows[:], ident[:])
-        nc.scalar.copy(vec_cols[:], banks[7][:, 0 : PACK + NT])
+        banks = [psum.tile([P, JW], F32, name=f"bank{b}") for b in range(BANKS)]
+        nc.tensor.transpose(banks[-1][:, 0:P], vec_rows[:], ident[:])
+        nc.scalar.copy(vec_cols[:], banks[-1][:, 0 : PACK + NT])
 
         nc.vector.tensor_copy(v_s[:], tab_s[:].bitcast(U8).indirect(offsets[:]))
-        nc.sync.dma_start(v_s1[0:112, :], v_s[4:116, :].bitcast(I32))
+        nc.sync.dma_start(v_s1[0:SHIFT_ROWS, :], v_s[PLANE_ROWS : PLANE_ROWS + SHIFT_ROWS, :].bitcast(I32))
 
         nc.vector.tensor_copy(
-            w_s[:].rearrange("p g (t b w) -> p g t b w", t=PACK, w=2),
-            w1s_host[:, 0 : PASSES * H // 2].rearrange("p (g b t w) -> p g t b w", g=2, t=PACK, w=2),
+            w_s[:].rearrange("p g (t b w) -> p g t b w", t=PACK, w=RUN // 4),
+            scale_stage[:, 0 : PASSES * H // 2].rearrange("p (g b t w) -> p g t b w", g=2, t=PACK, w=RUN // 4),
         )
         nc.vector.tensor_copy(
-            w1_c[:].rearrange("p t a (q w) -> p t (a q) w", w=4),
-            w1_raw[:].rearrange("p a (q t w) -> p t (a q) w", t=PACK, w=4),
+            w1_c[:].rearrange("p t a (b w) -> p t (a b) w", w=RUN // 2),
+            w1_raw[:].rearrange("p a (b t w) -> p t (a b) w", t=PACK, w=RUN // 2),
         )
+
+        half_bytes = PACK * NH * 4
         wl_raw = [
-            [placed([P, PACK, NH], F32, f"wl_raw{a}{hf}", (20 + 4 * (2 * a + hf)) * KIB) for hf in range(2)]
-            for a in range(PASSES)
+            [placed([P, PACK, NH], F32, f"wl_raw{a}{hf}", at + hf * half_bytes) for hf in range(2)]
+            for a, at in enumerate((AT_WL_FIRST_PASS, AT_WL_SECOND_PASS))
         ]
-        w2_raw = placed([P, PACK, N], F32, "w2_raw", 36 * KIB)
+        w2_raw = placed([P, PACK, N], F32, "w2_raw", AT_W2)
         wl_rows = wl.rearrange("(a p i) n -> a p i n", a=PASSES, i=PACK)
-        w2_rows = w2.rearrange("(q t i) n -> t q i n", t=PACK, i=8)
+        w2_rows = w2.rearrange("(b t i) n -> t b i n", t=PACK, i=RUN)
         wrs_rows = wr_scales.bitcast(I32).rearrange("a q c -> q a c")
         for a in range(PASSES):
             nc.sync.dma_start(wl_raw[a][0][:], wl_rows[a][:, :, 0:NH])
-        wr_c = placed([P, PASSES, N], I32, "wr_c", 16 * KIB)
+        wr_c = placed([P, PASSES, N], I32, "wr_c", AT_WR)
         nc.sync.dma_start(
             wr_c[:], wr_words.rearrange("a p c i -> a p (c i)").bitcast(I32).rearrange("a p c -> p a c")
         )
         for q in range(QUADS):
-            nc.sync.dma_start(wr_s[32 * q : 32 * q + 4, :, :], wrs_rows[4 * q : 4 * q + 4])
+            nc.sync.dma_start(
+                wr_s[32 * q : 32 * q + PLANE_ROWS, :, :], wrs_rows[PLANE_ROWS * q : PLANE_ROWS * (q + 1)]
+            )
         for t in range(PACK):
             nc.sync.dma_start(w2_raw[:, t, :], w2_rows[t])
         for a in range(PASSES):
             nc.sync.dma_start(wl_raw[a][1][:], wl_rows[a][:, :, NH:N])
 
         v_c = [
-            [placed([P, JW], U32, "v_c00", 13 * KIB), placed([P, JW], U32, "v_c01", 53 * KIB)],
+            [tile([P, JW], U32, "v_c00"), placed([P, JW], U32, "v_c01", AT_V01)],
             [tile([P, JW], U32, "v_c10"), tile([P, JW], U32, "v_c11")],
         ]
-        cols16 = JW // 16
+        list_cols = JW // 16
         for a in range(PASSES):
             for jb in range(JB):
                 nc.vector.tensor_copy(
                     v_c[a][jb][:],
-                    tab_w[a][:].bitcast(U32).indirect(offsets[:, jb * cols16 : (jb + 1) * cols16]),
+                    tab_w[a][:].bitcast(U32).indirect(offsets[:, jb * list_cols : (jb + 1) * list_cols]),
                 )
 
         def v_plane(a, jb):
-            return v_s[4 * a : P, jb * JW : (jb + 1) * JW]
+            return v_s[PLANE_ROWS * a : P, jb * JW : (jb + 1) * JW]
 
         def v_plane_from_zero(a, jb):
             if a == 0:
@@ -146,15 +171,20 @@ def tile_list_cardinality_error_kernel(
                 src.rearrange("p t (c i) -> p c t i", i=4),
             )
 
-        def quantize(grouped, name):
-            width = grouped.shape[1] // PACK
+        def grouped(copy, src, name, buffer):
+            dst = placed([P, PACK * src.shape[2]], BF16, name, AT_GROUP[buffer])
+            interleave(copy, dst[:], src)
+            return dst
+
+        def quantize(values, name):
+            width = values.shape[1] // PACK
             codes = tile([P, width], U32, name + "_c")
             scales = tile([P, width], U8, name + "_s")
-            nc.vector.quantize_mx(out=codes[:].bitcast(FP8X4), scales=scales[:], in_=grouped[:])
+            nc.vector.quantize_mx(out=codes[:].bitcast(FP8X4), scales=scales[:], in_=values[:])
             return codes, scales
 
-        wl_first = placed([P, PASSES * PACK * NH], BF16, "wl_first", 64 * KIB)
-        interleave(nc.scalar.copy, wl_first[:, 0 : PACK * NH], wl_raw[0][0][:])
+        wl_first = placed([P, PASSES * PACK * NH], BF16, "wl_first", AT_GROUP[0])
+
         h_rows = [tile([P, PACK, JW], BF16, f"h_rows{jb}") for jb in range(JB)]
         for jb in range(JB):
             for t in range(PACK):
@@ -174,17 +204,14 @@ def tile_list_cardinality_error_kernel(
 
         refs, h_q, wl_q, w2_q = {}, {}, {}, {}
 
-        def grouped(copy, src, name, kib):
-            dst = placed([P, PACK * src.shape[2]], BF16, name, (64 + kib) * KIB)
-            interleave(copy, dst[:], src)
-            return dst
-
+        def reference_bank(c, jb):
+            return banks[4 * jb + c % 2]
 
         def estimate_bank(c, jb):
             return banks[4 * jb + c % 2 + (2 if c < 2 else 0)]
 
         def reference_tile(c, jb):
-            acc = banks[4 * jb + c % 2]
+            acc = reference_bank(c, jb)
             for a in range(PASSES):
                 nc.tensor.matmul_mx(
                     out=acc[:],
@@ -199,7 +226,7 @@ def tile_list_cardinality_error_kernel(
             nc.scalar.activation(ref, acc[:], ACT.Copy, scale=vec_cols[:, PACK + c : PACK + c + 1])
             refs[(c, jb)] = ref
 
-        def error_tile(c, jb):
+        def estimate_tile(c, jb):
             hf, first = c // 2, (c % 2) * P
             acc = estimate_bank(c, jb)
             for a in range(PASSES):
@@ -237,33 +264,35 @@ def tile_list_cardinality_error_kernel(
                 nc.sync.dma_start(out[c * P : (c + 1) * P, jb * JW : (jb + 1) * JW][:, cols], err[:, cols])
 
         on_vector, on_scalar = nc.vector.tensor_copy, nc.scalar.copy
-        interleave(on_vector, wl_first[:, PACK * NH :], wl_raw[1][0][:])
-        h_first = grouped(on_vector, h_rows[0][:], "h_first", 4)
-        codes, scales = quantize(wl_first, "wl_first")
         for a in range(PASSES):
-            wl_q[(a, 0)] = (codes, scales, a * NH)
-        h_q[0] = quantize(h_first, "h_first")
+            interleave(on_vector, wl_first[:, a * PACK * NH : (a + 1) * PACK * NH], wl_raw[a][0][:])
+        wl_first_q = quantize(wl_first, "wl_first")
+        for a in range(PASSES):
+            wl_q[(a, 0)] = wl_first_q + (a * NH,)
+        h_first = grouped(on_vector, h_rows[0][:], "h_first", 1)
         w2_first = grouped(on_vector, w2_raw[:, :, 0:NH], "w2_first", 0)
+        h_q[0] = quantize(h_first, "h_first")
         w2_q[0] = quantize(w2_first, "w2_first")
         for c in (0, 1):
             reference_tile(c, 0)
-            error_tile(c, 0)
-        h_second = grouped(on_vector, h_rows[1][:], "h_second", 8)
+            estimate_tile(c, 0)
+        h_second = grouped(on_vector, h_rows[1][:], "h_second", 2)
+        wl_second0 = grouped(on_vector, wl_raw[0][1][:], "wl_second0", 0)
         h_q[1] = quantize(h_second, "h_second")
         for c in (0, 1):
             reference_tile(c, 1)
-            error_tile(c, 1)
+            estimate_tile(c, 1)
+
         second_half = ((2, 0), (3, 0), (2, 1), (3, 1))
-        wl_second0 = grouped(on_vector, wl_raw[0][1][:], "wl_second0", 0)
-        w2_second = grouped(on_vector, w2_raw[:, :, NH:N], "w2_second", 4)
-        wl_second1 = grouped(on_scalar, wl_raw[1][1][:], "wl_second1", 8)
+        wl_second1 = grouped(on_scalar, wl_raw[1][1][:], "wl_second1", 1)
+        w2_second = grouped(on_vector, w2_raw[:, :, NH:N], "w2_second", 2)
         for c, jb in second_half:
             reference_tile(c, jb)
         wl_q[(0, 1)] = quantize(wl_second0, "wl_second0") + (0,)
-        w2_q[1] = quantize(w2_second, "w2_second")
         wl_q[(1, 1)] = quantize(wl_second1, "wl_second1") + (0,)
+        w2_q[1] = quantize(w2_second, "w2_second")
         for c, jb in ((0, 0), (1, 0), (0, 1), (1, 1)):
             finish_tile(c, jb)
         for c, jb in second_half:
-            error_tile(c, jb)
+            estimate_tile(c, jb)
             finish_tile(c, jb, 2 if (c, jb) == second_half[-1] else 1)

@@ -26,22 +26,26 @@ NT = N // P
 NH = N // 2
 QUADS = 4
 PLANE_ROWS = 4
-SHIFT_ROWS = 112
+PASS_ROWS = 16
+SHIFT_ROWS = P - PASS_ROWS
 RUN = 8
 BANKS = 8
 KIB = 1024
 
-AT_TABLE1 = 2 * KIB
-AT_ZEROS_SECOND = 9 * KIB + 512
-AT_W1 = 11 * KIB
-AT_V01 = 12 * KIB
-AT_SCALE_STAGE = 13 * KIB
-AT_WR = 16 * KIB
-AT_WL_FIRST_PASS = 20 * KIB
-AT_WL_SECOND_PASS = 28 * KIB
-AT_W2 = 36 * KIB
-AT_TABLE0 = 45 * KIB
-AT_GROUP = (64 * KIB, 68 * KIB, 72 * KIB)
+AT_ZEROS_SECOND = 0
+AT_WL_EARLY = 0
+AT_TABLE1 = 4 * KIB
+AT_W1 = 12 * KIB
+AT_W1_SCALES = 14 * KIB
+AT_V01 = 13 * KIB
+AT_TABLE_SCALES = 16 * KIB
+AT_WR_SCALES = 17 * KIB
+AT_WL_NEXT = 18 * KIB
+AT_WR = 22 * KIB
+AT_W2 = 26 * KIB
+AT_WL_LATE = 34 * KIB
+AT_TABLE0 = 44 * KIB
+AT_W2_GROUPED = 56 * KIB
 
 
 def tile_list_cardinality_error_kernel(
@@ -60,11 +64,9 @@ def tile_list_cardinality_error_kernel(
             return shared.tile(shape, dtype, name=name, align_bytes=64, offset=offset)
 
         offsets = keep.tile([P, S // 16], U16, name="offsets")
-        tab_s = tile([P, T // 4], I32, "tab_s")
+        tab_s = placed([P, 26 * KIB // 4], I32, "tab_s", AT_TABLE_SCALES)[:, 0 : T // 4]
         w1_c = tile([P, PACK, PASSES, P // 2], I32, "w1_c")
-        w_s = tile([P, 2, PASSES * H // 4], I32, "w_s")
-        w1_s = w_s[:, 0, :].rearrange("p (t a m) -> p t a m", t=PACK, a=PASSES)
-        wr_s = w_s[:, 1, :].rearrange("p (a c) -> p a c", a=PASSES)
+        w1_s = tile([P, PACK, PASSES, P // 4], I32, "w1_s")
         v_s = tile([P, S], U8, "v_s")
         v_s1 = tile([P, S // 4], I32, "v_s1")
         vec_rows = tile([P, P], F32, "vec_rows")
@@ -72,70 +74,67 @@ def tile_list_cardinality_error_kernel(
         vec_cols = tile([P, PACK + NT], F32, "vec_cols")
 
         zeros_first = placed([P, P], F32, "zeros_first", AT_TABLE0)
-        zeros_second = placed([P, 2 * KIB // 4], I32, "zeros_second", AT_ZEROS_SECOND)
-        scale_stage = placed([P, 32 * KIB // 4], I32, "scale_stage", AT_SCALE_STAGE)
-        w1s_raw = scale_stage[:, 0 : PASSES * H // 4].rearrange("p (a c) -> p a c", a=PASSES)
+        zeros_second = placed([P, 14 * KIB // 4], I32, "zeros_second", AT_ZEROS_SECOND)[:, 0 : KIB // 4]
+        scale_stage = placed([P, PASSES * H // 4], I32, "scale_stage", AT_W1_SCALES)
+        w1s_raw = scale_stage[:].rearrange("p (a c) -> p a c", a=PASSES)
 
-        nc.vector.memset(tab_s[:], 0)
+        nc.vector.memset(tab_s, 0)
         nc.vector.memset(zeros_first[:], 0.0)
         nc.vector.tensor_copy(vec_rows[:], zeros_first[:])
-        nc.vector.memset(zeros_second[:], 0)
-        nc.vector.tensor_copy(scale_stage[:, 0 : PASSES * H // 2], zeros_second[:])
+        nc.vector.memset(zeros_second, 0)
+        nc.vector.tensor_copy(scale_stage[:], zeros_second)
         nc.vector.memset(v_s1[:], 0)
         make_identity(nc, ident[:])
 
         nc.sync.dma_start(offsets[:], offs)
-        tab_s_rows = tab_scales.bitcast(I32)
-        for q in range(QUADS):
-            nc.sync.dma_start(
-                tab_s[32 * q : 32 * q + PASSES * PLANE_ROWS, :],
-                tab_s_rows[:, PLANE_ROWS * q : PLANE_ROWS * (q + 1), :],
-            )
+        tab_s_rows = tab_scales.bitcast(I32).rearrange("a (q r) c -> r q a c", r=PLANE_ROWS)
+        for r in range(PLANE_ROWS):
+            nc.sync.dma_start(tab_s[r:P:PASS_ROWS, :], tab_s_rows[r])
         nc.sync.dma_start(vec_rows[0:PACK, :], b1.rearrange("(b t i) -> t b i", t=PACK, i=RUN))
         nc.sync.dma_start(vec_rows[PACK : PACK + NT, :], gr.rearrange("(c p) -> c p", p=P))
         tab_w_rows = tab_words.rearrange("a p t i -> a p (t i)").bitcast(I32)
         tab_w = [placed([P, T], I32, "tab_w0", AT_TABLE0), placed([P, T], I32, "tab_w1", AT_TABLE1)]
-        w1_raw = placed([P, PASSES, H // 2], I32, "w1_raw", AT_W1)
         nc.sync.dma_start(tab_w[0][:], tab_w_rows[0])
         w1s_rows = w1_scales.bitcast(I32).rearrange("a q c -> q a c")
         for q in range(QUADS):
             nc.sync.dma_start(
                 w1s_raw[32 * q : 32 * q + PLANE_ROWS, :, :], w1s_rows[PLANE_ROWS * q : PLANE_ROWS * (q + 1)]
             )
+        w1_raw = placed([P, PASSES, H // 2], I32, "w1_raw", AT_W1)
         nc.sync.dma_start(w1_raw[:], w1_words.bitcast(I32).rearrange("a p c -> p a c"))
         nc.sync.dma_start(tab_w[1][:], tab_w_rows[1])
+        wl_at = ((AT_WL_EARLY, AT_WL_LATE), (AT_WL_NEXT, AT_WL_LATE + PACK * NH * 4))
+        wl_raw = [
+            [placed([P, PACK, NH], F32, f"wl_raw{a}{hf}", wl_at[a][hf]) for hf in range(2)] for a in range(PASSES)
+        ]
+        wl_rows = wl.rearrange("(a p i) n -> a p i n", a=PASSES, i=PACK)
+        nc.sync.dma_start(wl_raw[0][0][:], wl_rows[0][:, :, 0:NH])
 
         banks = [psum.tile([P, JW], F32, name=f"bank{b}") for b in range(BANKS)]
         nc.tensor.transpose(banks[-1][:, 0:P], vec_rows[:], ident[:])
         nc.scalar.copy(vec_cols[:], banks[-1][:, 0 : PACK + NT])
 
-        nc.vector.tensor_copy(v_s[:], tab_s[:].bitcast(U8).indirect(offsets[:]))
-        nc.sync.dma_start(v_s1[0:SHIFT_ROWS, :], v_s[PLANE_ROWS : PLANE_ROWS + SHIFT_ROWS, :].bitcast(I32))
-
+        nc.vector.tensor_copy(v_s[:], tab_s.bitcast(U8).indirect(offsets[:]))
+        nc.sync.dma_start(v_s1[0:SHIFT_ROWS, :], v_s[PASS_ROWS:P, :].bitcast(I32))
         nc.vector.tensor_copy(
-            w_s[:].rearrange("p g (t b w) -> p g t b w", t=PACK, w=RUN // 4),
-            scale_stage[:, 0 : PASSES * H // 2].rearrange("p (g b t w) -> p g t b w", g=2, t=PACK, w=RUN // 4),
+            w1_s[:].rearrange("p t a (b w) -> p t (a b) w", w=RUN // 4),
+            w1s_raw.rearrange("p a (b t w) -> p t (a b) w", t=PACK, w=RUN // 4),
         )
         nc.vector.tensor_copy(
             w1_c[:].rearrange("p t a (b w) -> p t (a b) w", w=RUN // 2),
             w1_raw[:].rearrange("p a (b t w) -> p t (a b) w", t=PACK, w=RUN // 2),
         )
 
-        half_bytes = PACK * NH * 4
-        wl_raw = [
-            [placed([P, PACK, NH], F32, f"wl_raw{a}{hf}", at + hf * half_bytes) for hf in range(2)]
-            for a, at in enumerate((AT_WL_FIRST_PASS, AT_WL_SECOND_PASS))
-        ]
+        wr_s = placed([P, PASSES, N // 4], I32, "wr_s", AT_WR_SCALES)
+        nc.gpsimd.memset(wr_s[:], 0)
         w2_raw = placed([P, PACK, N], F32, "w2_raw", AT_W2)
-        wl_rows = wl.rearrange("(a p i) n -> a p i n", a=PASSES, i=PACK)
         w2_rows = w2.rearrange("(b t i) n -> t b i n", t=PACK, i=RUN)
-        wrs_rows = wr_scales.bitcast(I32).rearrange("a q c -> q a c")
-        for a in range(PASSES):
-            nc.sync.dma_start(wl_raw[a][0][:], wl_rows[a][:, :, 0:NH])
+        nc.sync.dma_start(wl_raw[1][0][:], wl_rows[1][:, :, 0:NH])
         wr_c = placed([P, PASSES, N], I32, "wr_c", AT_WR)
         nc.sync.dma_start(
             wr_c[:], wr_words.rearrange("a p c i -> a p (c i)").bitcast(I32).rearrange("a p c -> p a c")
         )
+        wrs_rows = wr_scales.bitcast(I32).rearrange("a q c -> q a c")
         for q in range(QUADS):
             nc.sync.dma_start(
                 wr_s[32 * q : 32 * q + PLANE_ROWS, :, :], wrs_rows[PLANE_ROWS * q : PLANE_ROWS * (q + 1)]
@@ -158,12 +157,7 @@ def tile_list_cardinality_error_kernel(
                 )
 
         def v_plane(a, jb):
-            return v_s[PLANE_ROWS * a : P, jb * JW : (jb + 1) * JW]
-
-        def v_plane_from_zero(a, jb):
-            if a == 0:
-                return v_plane(0, jb)
-            return v_s1[:].bitcast(U8)[:, jb * JW : (jb + 1) * JW]
+            return (v_s[:], v_s1[:].bitcast(U8))[a][:, jb * JW : (jb + 1) * JW]
 
         def interleave(copy, dst, src):
             copy(
@@ -171,8 +165,9 @@ def tile_list_cardinality_error_kernel(
                 src.rearrange("p t (c i) -> p c t i", i=4),
             )
 
-        def grouped(copy, src, name, buffer):
-            dst = placed([P, PACK * src.shape[2]], BF16, name, AT_GROUP[buffer])
+        def grouped(copy, src, name, at=None):
+            shape = [P, PACK * src.shape[2]]
+            dst = tile(shape, BF16, name) if at is None else placed(shape, BF16, name, at)
             interleave(copy, dst[:], src)
             return dst
 
@@ -182,8 +177,6 @@ def tile_list_cardinality_error_kernel(
             scales = tile([P, width], U8, name + "_s")
             nc.vector.quantize_mx(out=codes[:].bitcast(FP8X4), scales=scales[:], in_=values[:])
             return codes, scales
-
-        wl_first = placed([P, PASSES * PACK * NH], BF16, "wl_first", AT_GROUP[0])
 
         h_rows = [tile([P, PACK, JW], BF16, f"h_rows{jb}") for jb in range(JB)]
         for jb in range(JB):
@@ -196,7 +189,7 @@ def tile_list_cardinality_error_kernel(
                         lhsT=w1_c[:, t, a, :].bitcast(U8).bitcast(FP4X4),
                         lhsT_scale=w1_s[:, t, a, :].bitcast(U8),
                         rhs=v_c[a][jb][:].bitcast(FP8X4),
-                        rhs_scale=v_plane_from_zero(a, jb),
+                        rhs_scale=v_plane(a, jb),
                         start=(a == order[0]),
                         stop=(a == order[-1]),
                     )
@@ -204,14 +197,8 @@ def tile_list_cardinality_error_kernel(
 
         refs, h_q, wl_q, w2_q = {}, {}, {}, {}
 
-        def reference_bank(c, jb):
-            return banks[4 * jb + c % 2]
-
-        def estimate_bank(c, jb):
-            return banks[4 * jb + c % 2 + (2 if c < 2 else 0)]
-
         def reference_tile(c, jb):
-            acc = reference_bank(c, jb)
+            acc = banks[NT * jb + c]
             for a in range(PASSES):
                 nc.tensor.matmul_mx(
                     out=acc[:],
@@ -228,10 +215,10 @@ def tile_list_cardinality_error_kernel(
 
         def estimate_tile(c, jb):
             hf, first = c // 2, (c % 2) * P
-            acc = estimate_bank(c, jb)
+            acc = banks[NT * jb + c]
             for a in range(PASSES):
-                codes, scales, base = wl_q[(a, hf)]
-                cols = slice(base + first, base + first + P)
+                codes, scales = wl_q[(a, hf)]
+                cols = slice(first, first + P)
                 nc.tensor.matmul_mx(
                     out=acc[:],
                     lhsT=codes[:, cols].bitcast(FP8X4),
@@ -253,7 +240,7 @@ def tile_list_cardinality_error_kernel(
             )
 
         def finish_tile(c, jb, pieces=1):
-            acc = estimate_bank(c, jb)
+            acc = banks[NT * jb + c]
             diff = tile([P, JW], F32, f"diff{c}{jb}")
             err = tile([P, JW], F32, f"err{c}{jb}")
             width = JW // pieces
@@ -264,35 +251,43 @@ def tile_list_cardinality_error_kernel(
                 nc.sync.dma_start(out[c * P : (c + 1) * P, jb * JW : (jb + 1) * JW][:, cols], err[:, cols])
 
         on_vector, on_scalar = nc.vector.tensor_copy, nc.scalar.copy
-        for a in range(PASSES):
-            interleave(on_vector, wl_first[:, a * PACK * NH : (a + 1) * PACK * NH], wl_raw[a][0][:])
-        wl_first_q = quantize(wl_first, "wl_first")
-        for a in range(PASSES):
-            wl_q[(a, 0)] = wl_first_q + (a * NH,)
-        h_first = grouped(on_vector, h_rows[0][:], "h_first", 1)
-        w2_first = grouped(on_vector, w2_raw[:, :, 0:NH], "w2_first", 0)
+
+        def grouped_on_gpsimd(src, name):
+            dst = tile([P, PACK * NH], BF16, name)
+            nc.gpsimd.tensor_scalar(
+                dst[:].rearrange("p (c t) -> p c t", t=PACK), src.rearrange("p t c -> p c t"), 1.0, 0.0, ALU.mult, ALU.add
+            )
+            return dst
+
+        wl00 = grouped_on_gpsimd(wl_raw[0][0][:], "wl00")
+        wl10 = grouped(on_vector, wl_raw[1][0][:], "wl10")
+        wl_q[(0, 0)] = quantize(wl00, "wl00")
+        wl_q[(1, 0)] = quantize(wl10, "wl10")
+        h_first = grouped(on_vector, h_rows[0][:], "h_first", AT_WL_NEXT)
         h_q[0] = quantize(h_first, "h_first")
+        w2_first = grouped(on_vector, w2_raw[:, :, 0:NH], "w2_first", AT_W2_GROUPED)
+        w2_second = grouped(on_vector, w2_raw[:, :, NH:N], "w2_second")
         w2_q[0] = quantize(w2_first, "w2_first")
-        for c in (0, 1):
-            reference_tile(c, 0)
-            estimate_tile(c, 0)
-        h_second = grouped(on_vector, h_rows[1][:], "h_second", 2)
-        wl_second0 = grouped(on_vector, wl_raw[0][1][:], "wl_second0", 0)
+        h_second = grouped(on_vector, h_rows[1][:], "h_second", AT_W2_GROUPED)
+        w2_q[1] = quantize(w2_second, "w2_second")
         h_q[1] = quantize(h_second, "h_second")
+        for c in range(NT):
+            reference_tile(c, 0)
         for c in (0, 1):
             reference_tile(c, 1)
+        for c in (0, 1):
+            estimate_tile(c, 0)
+        wl11 = grouped(on_scalar, wl_raw[1][1][:], "wl11")
+        for c in (2, 3):
+            reference_tile(c, 1)
+        for c in (0, 1):
             estimate_tile(c, 1)
-
-        second_half = ((2, 0), (3, 0), (2, 1), (3, 1))
-        wl_second1 = grouped(on_scalar, wl_raw[1][1][:], "wl_second1", 1)
-        w2_second = grouped(on_vector, w2_raw[:, :, NH:N], "w2_second", 2)
-        for c, jb in second_half:
-            reference_tile(c, jb)
-        wl_q[(0, 1)] = quantize(wl_second0, "wl_second0") + (0,)
-        wl_q[(1, 1)] = quantize(wl_second1, "wl_second1") + (0,)
-        w2_q[1] = quantize(w2_second, "w2_second")
+        wl01 = grouped(on_vector, wl_raw[0][1][:], "wl01")
+        wl_q[(0, 1)] = quantize(wl01, "wl01")
+        wl_q[(1, 1)] = quantize(wl11, "wl11")
         for c, jb in ((0, 0), (1, 0), (0, 1), (1, 1)):
             finish_tile(c, jb)
+        second_half = ((2, 0), (3, 0), (2, 1), (3, 1))
         for c, jb in second_half:
             estimate_tile(c, jb)
             finish_tile(c, jb, 2 if (c, jb) == second_half[-1] else 1)

@@ -33,19 +33,17 @@ BANKS = 8
 KIB = 1024
 
 AT_ZEROS_SECOND = 0
-AT_WL_EARLY = 0
-AT_TABLE1 = 4 * KIB
-AT_W1 = 12 * KIB
-AT_W1_SCALES = 14 * KIB
-AT_V01 = 13 * KIB
-AT_TABLE_SCALES = 16 * KIB
-AT_WR_SCALES = 17 * KIB
-AT_WL_NEXT = 18 * KIB
+AT_TABLE1 = 0
+AT_W1 = 8 * KIB
+AT_W1_SCALES = 10 * KIB
+AT_V01 = 9 * KIB
+AT_TABLE_SCALES = 12 * KIB
+AT_WR_SCALES = 13 * KIB
+AT_WL = (14 * KIB, 34 * KIB)
 AT_WR = 22 * KIB
 AT_W2 = 26 * KIB
-AT_WL_LATE = 34 * KIB
+AT_H1 = 56 * KIB
 AT_TABLE0 = 44 * KIB
-AT_W2_GROUPED = 56 * KIB
 
 
 def tile_list_cardinality_error_kernel(
@@ -64,7 +62,7 @@ def tile_list_cardinality_error_kernel(
             return shared.tile(shape, dtype, name=name, align_bytes=64, offset=offset)
 
         offsets = keep.tile([P, S // 16], U16, name="offsets")
-        tab_s = placed([P, 26 * KIB // 4], I32, "tab_s", AT_TABLE_SCALES)[:, 0 : T // 4]
+        tab_s = placed([P, 30 * KIB // 4], I32, "tab_s", AT_TABLE_SCALES)[:, 0 : T // 4]
         w1_c = tile([P, PACK, PASSES, P // 2], I32, "w1_c")
         w1_s = tile([P, PACK, PASSES, P // 4], I32, "w1_s")
         v_s = tile([P, S], U8, "v_s")
@@ -74,7 +72,7 @@ def tile_list_cardinality_error_kernel(
         vec_cols = tile([P, PACK + NT], F32, "vec_cols")
 
         zeros_first = placed([P, P], F32, "zeros_first", AT_TABLE0)
-        zeros_second = placed([P, 14 * KIB // 4], I32, "zeros_second", AT_ZEROS_SECOND)[:, 0 : KIB // 4]
+        zeros_second = placed([P, 10 * KIB // 4], I32, "zeros_second", AT_ZEROS_SECOND)[:, 0 : KIB // 4]
         scale_stage = placed([P, PASSES * H // 4], I32, "scale_stage", AT_W1_SCALES)
         w1s_raw = scale_stage[:].rearrange("p (a c) -> p a c", a=PASSES)
 
@@ -103,12 +101,6 @@ def tile_list_cardinality_error_kernel(
         w1_raw = placed([P, PASSES, H // 2], I32, "w1_raw", AT_W1)
         nc.sync.dma_start(w1_raw[:], w1_words.bitcast(I32).rearrange("a p c -> p a c"))
         nc.sync.dma_start(tab_w[1][:], tab_w_rows[1])
-        wl_at = ((AT_WL_EARLY, AT_WL_LATE), (AT_WL_NEXT, AT_WL_LATE + PACK * NH * 4))
-        wl_raw = [
-            [placed([P, PACK, NH], F32, f"wl_raw{a}{hf}", wl_at[a][hf]) for hf in range(2)] for a in range(PASSES)
-        ]
-        wl_rows = wl.rearrange("(a p i) n -> a p i n", a=PASSES, i=PACK)
-        nc.sync.dma_start(wl_raw[0][0][:], wl_rows[0][:, :, 0:NH])
 
         banks = [psum.tile([P, JW], F32, name=f"bank{b}") for b in range(BANKS)]
         nc.tensor.transpose(banks[-1][:, 0:P], vec_rows[:], ident[:])
@@ -129,7 +121,9 @@ def tile_list_cardinality_error_kernel(
         nc.gpsimd.memset(wr_s[:], 0)
         w2_raw = placed([P, PACK, N], F32, "w2_raw", AT_W2)
         w2_rows = w2.rearrange("(b t i) n -> t b i n", t=PACK, i=RUN)
-        nc.sync.dma_start(wl_raw[1][0][:], wl_rows[1][:, :, 0:NH])
+        wl_raw = [placed([P, PACK, N], F32, f"wl_raw{a}", AT_WL[a]) for a in range(PASSES)]
+        wl_rows = wl.rearrange("(a p i) n -> a p i n", a=PASSES, i=PACK)
+        nc.sync.dma_start(wl_raw[0][:], wl_rows[0])
         wr_c = placed([P, PASSES, N], I32, "wr_c", AT_WR)
         nc.sync.dma_start(
             wr_c[:], wr_words.rearrange("a p c i -> a p (c i)").bitcast(I32).rearrange("a p c -> p a c")
@@ -141,8 +135,7 @@ def tile_list_cardinality_error_kernel(
             )
         for t in range(PACK):
             nc.sync.dma_start(w2_raw[:, t, :], w2_rows[t])
-        for a in range(PASSES):
-            nc.sync.dma_start(wl_raw[a][1][:], wl_rows[a][:, :, NH:N])
+        nc.sync.dma_start(wl_raw[1][:], wl_rows[1])
 
         v_c = [
             [tile([P, JW], U32, "v_c00"), placed([P, JW], U32, "v_c01", AT_V01)],
@@ -214,30 +207,25 @@ def tile_list_cardinality_error_kernel(
             refs[(c, jb)] = ref
 
         def estimate_tile(c, jb):
-            hf, first = c // 2, (c % 2) * P
-            acc = banks[NT * jb + c]
-            for a in range(PASSES):
-                codes, scales = wl_q[(a, hf)]
-                cols = slice(first, first + P)
-                nc.tensor.matmul_mx(
-                    out=acc[:],
-                    lhsT=codes[:, cols].bitcast(FP8X4),
-                    lhsT_scale=scales[:, cols],
-                    rhs=v_c[a][jb][:].bitcast(FP8X4),
-                    rhs_scale=v_plane(a, jb),
-                    start=(a == 0),
-                    stop=False,
-                )
-            codes, scales = w2_q[hf]
-            nc.tensor.matmul_mx(
-                out=acc[:],
-                lhsT=codes[:, first : first + P].bitcast(FP8X4),
-                lhsT_scale=scales[:, first : first + P],
-                rhs=h_q[jb][0][:].bitcast(FP8X4),
-                rhs_scale=h_q[jb][1][:],
-                start=False,
-                stop=True,
+            def columns(operand, first):
+                codes, scales = operand
+                return codes[:, first : first + P].bitcast(FP8X4), scales[:, first : first + P]
+
+            passes = (
+                columns(wl_q[0], c * P) + (v_c[0][jb][:], v_plane(0, jb)),
+                columns(w2_q[0], c * P) + (h_q[jb][0][:], h_q[jb][1][:]),
+                columns(wl_q[1 + c // 2], (c % 2) * P) + (v_c[1][jb][:], v_plane(1, jb)),
             )
+            for n, (codes, scales, moving, moving_scales) in enumerate(passes):
+                nc.tensor.matmul_mx(
+                    out=banks[NT * jb + c][:],
+                    lhsT=codes,
+                    lhsT_scale=scales,
+                    rhs=moving.bitcast(FP8X4),
+                    rhs_scale=moving_scales,
+                    start=(n == 0),
+                    stop=(n == len(passes) - 1),
+                )
 
         def finish_tile(c, jb, pieces=1):
             acc = banks[NT * jb + c]
@@ -252,39 +240,27 @@ def tile_list_cardinality_error_kernel(
 
         on_vector, on_scalar = nc.vector.tensor_copy, nc.scalar.copy
 
-        def grouped_on_gpsimd(src, name):
-            dst = tile([P, PACK * NH], BF16, name)
-            nc.gpsimd.tensor_scalar(
-                dst[:].rearrange("p (c t) -> p c t", t=PACK), src.rearrange("p t c -> p c t"), 1.0, 0.0, ALU.mult, ALU.add
-            )
-            return dst
-
-        wl00 = grouped_on_gpsimd(wl_raw[0][0][:], "wl00")
-        wl10 = grouped(on_vector, wl_raw[1][0][:], "wl10")
-        wl_q[(0, 0)] = quantize(wl00, "wl00")
-        wl_q[(1, 0)] = quantize(wl10, "wl10")
-        h_first = grouped(on_vector, h_rows[0][:], "h_first", AT_WL_NEXT)
+        wl0 = grouped(on_vector, wl_raw[0][:], "wl0")
+        wl_q[0] = quantize(wl0, "wl0")
+        h_first = grouped(on_vector, h_rows[0][:], "h_first", AT_WL[0])
+        w2_all = grouped(on_vector, w2_raw[:], "w2_all", AT_H1)
         h_q[0] = quantize(h_first, "h_first")
-        w2_first = grouped(on_vector, w2_raw[:, :, 0:NH], "w2_first", AT_W2_GROUPED)
-        w2_second = grouped(on_vector, w2_raw[:, :, NH:N], "w2_second")
-        w2_q[0] = quantize(w2_first, "w2_first")
-        h_second = grouped(on_vector, h_rows[1][:], "h_second", AT_W2_GROUPED)
-        w2_q[1] = quantize(w2_second, "w2_second")
+        w2_q[0] = quantize(w2_all, "w2_all")
+        wl10 = grouped(on_vector, wl_raw[1][:, :, 0:NH], "wl10")
+        h_second = grouped(on_vector, h_rows[1][:], "h_second", AT_H1)
+        wl_q[1] = quantize(wl10, "wl10")
         h_q[1] = quantize(h_second, "h_second")
         for c in range(NT):
             reference_tile(c, 0)
         for c in (0, 1):
             reference_tile(c, 1)
-        for c in (0, 1):
-            estimate_tile(c, 0)
-        wl11 = grouped(on_scalar, wl_raw[1][1][:], "wl11")
+        wl11 = grouped(on_scalar, wl_raw[1][:, :, NH:N], "wl11")
         for c in (2, 3):
             reference_tile(c, 1)
-        for c in (0, 1):
-            estimate_tile(c, 1)
-        wl01 = grouped(on_vector, wl_raw[0][1][:], "wl01")
-        wl_q[(0, 1)] = quantize(wl01, "wl01")
-        wl_q[(1, 1)] = quantize(wl11, "wl11")
+        for jb in range(JB):
+            for c in (0, 1):
+                estimate_tile(c, jb)
+        wl_q[2] = quantize(wl11, "wl11")
         for c, jb in ((0, 0), (1, 0), (0, 1), (1, 1)):
             finish_tile(c, jb)
         second_half = ((2, 0), (3, 0), (2, 1), (3, 1))

@@ -31,19 +31,22 @@ SHIFT_ROWS = P - PASS_ROWS
 RUN = 8
 BANKS = 8
 KIB = 1024
+WARM_UP_PASSES = 2
 
 AT_ZEROS_SECOND = 0
-AT_TABLE1 = 0
-AT_W1 = 8 * KIB
-AT_W1_SCALES = 10 * KIB
-AT_V01 = 9 * KIB
-AT_TABLE_SCALES = 12 * KIB
-AT_WR_SCALES = 13 * KIB
-AT_WL = (14 * KIB, 34 * KIB)
+AT_WL_EARLY = 0
+AT_TABLE1 = 4 * KIB
+AT_W1 = 12 * KIB
+AT_W1_SCALES = 14 * KIB
+AT_V01 = 13 * KIB
+AT_TABLE_SCALES = 16 * KIB
+AT_WR_SCALES = 17 * KIB
+AT_WL_NEXT = 18 * KIB
 AT_WR = 22 * KIB
 AT_W2 = 26 * KIB
-AT_H1 = 56 * KIB
+AT_WL_LATE = 34 * KIB
 AT_TABLE0 = 44 * KIB
+AT_H1 = 56 * KIB
 
 
 def tile_list_cardinality_error_kernel(
@@ -62,7 +65,7 @@ def tile_list_cardinality_error_kernel(
             return shared.tile(shape, dtype, name=name, align_bytes=64, offset=offset)
 
         offsets = keep.tile([P, S // 16], U16, name="offsets")
-        tab_s = placed([P, 30 * KIB // 4], I32, "tab_s", AT_TABLE_SCALES)[:, 0 : T // 4]
+        tab_s = placed([P, 26 * KIB // 4], I32, "tab_s", AT_TABLE_SCALES)[:, 0 : T // 4]
         w1_c = tile([P, PACK, PASSES, P // 2], I32, "w1_c")
         w1_s = tile([P, PACK, PASSES, P // 4], I32, "w1_s")
         v_s = tile([P, S], U8, "v_s")
@@ -72,7 +75,7 @@ def tile_list_cardinality_error_kernel(
         vec_cols = tile([P, PACK + NT], F32, "vec_cols")
 
         zeros_first = placed([P, P], F32, "zeros_first", AT_TABLE0)
-        zeros_second = placed([P, 10 * KIB // 4], I32, "zeros_second", AT_ZEROS_SECOND)[:, 0 : KIB // 4]
+        zeros_second = placed([P, 14 * KIB // 4], I32, "zeros_second", AT_ZEROS_SECOND)[:, 0 : KIB // 4]
         scale_stage = placed([P, PASSES * H // 4], I32, "scale_stage", AT_W1_SCALES)
         w1s_raw = scale_stage[:].rearrange("p (a c) -> p a c", a=PASSES)
 
@@ -101,6 +104,9 @@ def tile_list_cardinality_error_kernel(
         w1_raw = placed([P, PASSES, H // 2], I32, "w1_raw", AT_W1)
         nc.sync.dma_start(w1_raw[:], w1_words.bitcast(I32).rearrange("a p c -> p a c"))
         nc.sync.dma_start(tab_w[1][:], tab_w_rows[1])
+        wl_rows = wl.rearrange("(a p i) n -> a p i n", a=PASSES, i=PACK)
+        wl_early = placed([P, PACK, NH], F32, "wl_early", AT_WL_EARLY)
+        nc.sync.dma_start(wl_early[:], wl_rows[0][:, :, 0:NH])
 
         banks = [psum.tile([P, JW], F32, name=f"bank{b}") for b in range(BANKS)]
         nc.tensor.transpose(banks[-1][:, 0:P], vec_rows[:], ident[:])
@@ -121,9 +127,9 @@ def tile_list_cardinality_error_kernel(
         nc.gpsimd.memset(wr_s[:], 0)
         w2_raw = placed([P, PACK, N], F32, "w2_raw", AT_W2)
         w2_rows = w2.rearrange("(b t i) n -> t b i n", t=PACK, i=RUN)
-        wl_raw = [placed([P, PACK, N], F32, f"wl_raw{a}", AT_WL[a]) for a in range(PASSES)]
-        wl_rows = wl.rearrange("(a p i) n -> a p i n", a=PASSES, i=PACK)
-        nc.sync.dma_start(wl_raw[0][:], wl_rows[0])
+        wl_next = placed([P, PACK, NH], F32, "wl_next", AT_WL_NEXT)
+        wl_late = placed([P, PACK, N], F32, "wl_late", AT_WL_LATE)
+        nc.sync.dma_start(wl_next[:], wl_rows[0][:, :, NH:N])
         wr_c = placed([P, PASSES, N], I32, "wr_c", AT_WR)
         nc.sync.dma_start(
             wr_c[:], wr_words.rearrange("a p c i -> a p (c i)").bitcast(I32).rearrange("a p c -> p a c")
@@ -135,7 +141,7 @@ def tile_list_cardinality_error_kernel(
             )
         for t in range(PACK):
             nc.sync.dma_start(w2_raw[:, t, :], w2_rows[t])
-        nc.sync.dma_start(wl_raw[1][:], wl_rows[1])
+        nc.sync.dma_start(wl_late[:], wl_rows[1])
 
         v_c = [
             [tile([P, JW], U32, "v_c00"), placed([P, JW], U32, "v_c01", AT_V01)],
@@ -171,11 +177,22 @@ def tile_list_cardinality_error_kernel(
             nc.vector.quantize_mx(out=codes[:].bitcast(FP8X4), scales=scales[:], in_=values[:])
             return codes, scales
 
+        for n in range(WARM_UP_PASSES):
+            nc.tensor.matmul_mx(
+                out=banks[-1][:],
+                lhsT=tab_w[0][:, 0:P].bitcast(FP8X4),
+                lhsT_scale=v_s[:, 0:P],
+                rhs=tab_w[0][:, 0:JW].bitcast(FP8X4),
+                rhs_scale=v_s[:, 0:JW],
+                start=True,
+                stop=True,
+            )
+
         h_rows = [tile([P, PACK, JW], BF16, f"h_rows{jb}") for jb in range(JB)]
         for jb in range(JB):
             for t in range(PACK):
                 acc = banks[PACK * jb + t]
-                order = (0, 1) if jb == 0 else (1, 0)
+                order = (0, 1)
                 for a in order:
                     nc.tensor.matmul_mx(
                         out=acc[:],
@@ -186,7 +203,11 @@ def tile_list_cardinality_error_kernel(
                         start=(a == order[0]),
                         stop=(a == order[-1]),
                     )
-                nc.scalar.activation(h_rows[jb][:, t, :], acc[:], ACT.Relu, bias=vec_cols[:, t : t + 1])
+                bias = vec_cols[:, t : t + 1]
+                if (jb, t) == (0, PACK - 1):
+                    nc.vector.tensor_scalar(h_rows[jb][:, t, :], acc[:], bias, 0.0, ALU.add, ALU.max)
+                else:
+                    nc.scalar.activation(h_rows[jb][:, t, :], acc[:], ACT.Relu, bias=bias)
 
         refs, h_q, wl_q, w2_q = {}, {}, {}, {}
 
@@ -213,7 +234,7 @@ def tile_list_cardinality_error_kernel(
 
             passes = (
                 columns(wl_q[0], c * P) + (v_c[0][jb][:], v_plane(0, jb)),
-                columns(w2_q[0], c * P) + (h_q[jb][0][:], h_q[jb][1][:]),
+                columns(w2_q[c // 2], (c % 2) * P) + (h_q[jb][0][:], h_q[jb][1][:]),
                 columns(wl_q[1 + c // 2], (c % 2) * P) + (v_c[1][jb][:], v_plane(1, jb)),
             )
             for n, (codes, scales, moving, moving_scales) in enumerate(passes):
@@ -240,21 +261,32 @@ def tile_list_cardinality_error_kernel(
 
         on_vector, on_scalar = nc.vector.tensor_copy, nc.scalar.copy
 
-        wl0 = grouped(on_vector, wl_raw[0][:], "wl0")
+        wl0 = tile([P, PACK * N], BF16, "wl0")
+        nc.gpsimd.tensor_scalar(
+            wl0[:, 0 : PACK * NH].rearrange("p (c t) -> p c t", t=PACK),
+            wl_early[:].rearrange("p t c -> p c t"),
+            1.0,
+            0.0,
+            ALU.mult,
+            ALU.add,
+        )
+        interleave(on_vector, wl0[:, PACK * NH : PACK * N], wl_next[:])
+        h_first = grouped(on_vector, h_rows[0][:], "h_first", AT_WL_NEXT)
         wl_q[0] = quantize(wl0, "wl0")
-        h_first = grouped(on_vector, h_rows[0][:], "h_first", AT_WL[0])
-        w2_all = grouped(on_vector, w2_raw[:], "w2_all", AT_H1)
         h_q[0] = quantize(h_first, "h_first")
-        w2_q[0] = quantize(w2_all, "w2_all")
-        wl10 = grouped(on_vector, wl_raw[1][:, :, 0:NH], "wl10")
+        w2_first = grouped(on_vector, w2_raw[:, :, 0:NH], "w2_first", AT_H1)
+        w2_second = grouped(on_vector, w2_raw[:, :, NH:N], "w2_second")
+        w2_q[0] = quantize(w2_first, "w2_first")
+        w2_q[1] = quantize(w2_second, "w2_second")
         h_second = grouped(on_vector, h_rows[1][:], "h_second", AT_H1)
-        wl_q[1] = quantize(wl10, "wl10")
+        wl10 = grouped(on_vector, wl_late[:, :, 0:NH], "wl10")
         h_q[1] = quantize(h_second, "h_second")
+        wl_q[1] = quantize(wl10, "wl10")
         for c in range(NT):
             reference_tile(c, 0)
         for c in (0, 1):
             reference_tile(c, 1)
-        wl11 = grouped(on_scalar, wl_raw[1][:, :, NH:N], "wl11")
+        wl11 = grouped(on_scalar, wl_late[:, :, NH:N], "wl11")
         for c in (2, 3):
             reference_tile(c, 1)
         for jb in range(JB):
@@ -266,4 +298,4 @@ def tile_list_cardinality_error_kernel(
         second_half = ((2, 0), (3, 0), (2, 1), (3, 1))
         for c, jb in second_half:
             estimate_tile(c, jb)
-            finish_tile(c, jb, 2 if (c, jb) == second_half[-1] else 1)
+            finish_tile(c, jb, 2 if jb == 1 else 1)

@@ -31,7 +31,6 @@ SHIFT_ROWS = P - PASS_ROWS
 RUN = 8
 BANKS = 8
 KIB = 1024
-WARM_UP_PASSES = 2
 
 AT_ZEROS_SECOND = 0
 AT_WL_EARLY = 0
@@ -176,17 +175,6 @@ def tile_list_cardinality_error_kernel(
             scales = tile([P, width], U8, name + "_s")
             nc.vector.quantize_mx(out=codes[:].bitcast(FP8X4), scales=scales[:], in_=values[:])
             return codes, scales
-
-        for n in range(WARM_UP_PASSES):
-            nc.tensor.matmul_mx(
-                out=banks[-1][:],
-                lhsT=tab_w[0][:, 0:P].bitcast(FP8X4),
-                lhsT_scale=v_s[:, 0:P],
-                rhs=tab_w[0][:, 0:JW].bitcast(FP8X4),
-                rhs_scale=v_s[:, 0:JW],
-                start=True,
-                stop=True,
-            )
 
         h_rows = [tile([P, PACK, JW], BF16, f"h_rows{jb}") for jb in range(JB)]
         for jb in range(JB):

@@ -45,7 +45,6 @@ AT_WR = 22 * KIB
 AT_W2 = 26 * KIB
 AT_WL_LATE = 34 * KIB
 AT_TABLE0 = 44 * KIB
-AT_H1 = 56 * KIB
 
 
 def tile_list_cardinality_error_kernel(
@@ -127,7 +126,7 @@ def tile_list_cardinality_error_kernel(
         w2_raw = placed([P, PACK, N], F32, "w2_raw", AT_W2)
         w2_rows = w2.rearrange("(b t i) n -> t b i n", t=PACK, i=RUN)
         wl_next = placed([P, PACK, NH], F32, "wl_next", AT_WL_NEXT)
-        wl_late = placed([P, PACK, N], F32, "wl_late", AT_WL_LATE)
+        wl_late = [placed([P, PACK, NH], F32, f"wl_late{u}", AT_WL_LATE + 4 * KIB * u) for u in range(2)]
         nc.sync.dma_start(wl_next[:], wl_rows[0][:, :, NH:N])
         wr_c = placed([P, PASSES, N], I32, "wr_c", AT_WR)
         nc.sync.dma_start(
@@ -140,7 +139,8 @@ def tile_list_cardinality_error_kernel(
             )
         for t in range(PACK):
             nc.sync.dma_start(w2_raw[:, t, :], w2_rows[t])
-        nc.sync.dma_start(wl_late[:], wl_rows[1])
+        for u in range(2):
+            nc.sync.dma_start(wl_late[u][:], wl_rows[1][:, :, u * NH : (u + 1) * NH])
 
         v_c = [
             [tile([P, JW], U32, "v_c00"), placed([P, JW], U32, "v_c01", AT_V01)],
@@ -169,9 +169,9 @@ def tile_list_cardinality_error_kernel(
             interleave(copy, dst[:], src)
             return dst
 
-        def quantize(values, name):
+        def quantize(values, name, at=None):
             width = values.shape[1] // PACK
-            codes = tile([P, width], U32, name + "_c")
+            codes = tile([P, width], U32, name + "_c") if at is None else placed([P, width], U32, name + "_c", at)
             scales = tile([P, width], U8, name + "_s")
             nc.vector.quantize_mx(out=codes[:].bitcast(FP8X4), scales=scales[:], in_=values[:])
             return codes, scales
@@ -262,27 +262,29 @@ def tile_list_cardinality_error_kernel(
         h_first = grouped(on_vector, h_rows[0][:], "h_first", AT_WL_NEXT)
         wl_q[0] = quantize(wl0, "wl0")
         h_q[0] = quantize(h_first, "h_first")
-        w2_first = grouped(on_vector, w2_raw[:, :, 0:NH], "w2_first", AT_H1)
-        w2_second = grouped(on_vector, w2_raw[:, :, NH:N], "w2_second")
-        w2_q[0] = quantize(w2_first, "w2_first")
-        w2_q[1] = quantize(w2_second, "w2_second")
-        h_second = grouped(on_vector, h_rows[1][:], "h_second", AT_H1)
-        wl10 = grouped(on_vector, wl_late[:, :, 0:NH], "wl10")
-        h_q[1] = quantize(h_second, "h_second")
+        w2_first = grouped(on_vector, w2_raw[:, :, 0:NH], "w2_first")
+        h_second = grouped(on_vector, h_rows[1][:], "h_second")
+        wl10 = grouped(on_vector, wl_late[0][:], "wl10")
+        w2_q[0] = quantize(w2_first, "w2_first", AT_WL_LATE)
+        h_q[1] = quantize(h_second, "h_second", AT_WL_LATE + KIB)
         wl_q[1] = quantize(wl10, "wl10")
         for c in range(NT):
             reference_tile(c, 0)
+        w2_second = grouped(on_scalar, w2_raw[:, :, NH:N], "w2_second")
         for c in (0, 1):
             reference_tile(c, 1)
-        wl11 = grouped(on_scalar, wl_late[:, :, NH:N], "wl11")
+        wl11 = grouped(on_scalar, wl_late[1][:], "wl11")
         for c in (2, 3):
             reference_tile(c, 1)
         for jb in range(JB):
             for c in (0, 1):
                 estimate_tile(c, jb)
+        w2_q[1] = quantize(w2_second, "w2_second")
+        finish_tile(0, 0)
+        finish_tile(1, 0)
         wl_q[2] = quantize(wl11, "wl11")
-        for c, jb in ((0, 0), (1, 0), (0, 1), (1, 1)):
-            finish_tile(c, jb)
+        finish_tile(0, 1)
+        finish_tile(1, 1)
         second_half = ((2, 0), (3, 0), (2, 1), (3, 1))
         for c, jb in second_half:
             estimate_tile(c, jb)

@@ -31,6 +31,7 @@ SHIFT_ROWS = P - PASS_ROWS
 RUN = 8
 BANKS = 8
 KIB = 1024
+EARLY_SUMS = 5
 
 AT_ZEROS_SECOND = 0
 AT_WL_EARLY = 0
@@ -180,7 +181,7 @@ def tile_list_cardinality_error_kernel(
         for jb in range(JB):
             for t in range(PACK):
                 acc = banks[PACK * jb + t]
-                order = (0, 1)
+                order = (1, 0) if PACK * jb + t >= EARLY_SUMS else (0, 1)
                 for a in order:
                     nc.tensor.matmul_mx(
                         out=acc[:],

@@ -31,14 +31,14 @@ SHIFT_ROWS = P - PASS_ROWS
 RUN = 8
 BANKS = 8
 KIB = 1024
-EARLY_SUMS = 5
+EARLY_SUMS = 4
 
 AT_ZEROS_SECOND = 0
 AT_WL_EARLY = 0
 AT_TABLE1 = 4 * KIB
-AT_W1 = 12 * KIB
-AT_W1_SCALES = 14 * KIB
-AT_V01 = 13 * KIB
+AT_W1 = (12 * KIB, 14 * KIB)
+AT_V01 = 12 * KIB
+AT_W1_SCALES = 15 * KIB
 AT_TABLE_SCALES = 16 * KIB
 AT_WR_SCALES = 17 * KIB
 AT_WL_NEXT = 18 * KIB
@@ -46,6 +46,7 @@ AT_WR = 22 * KIB
 AT_W2 = 26 * KIB
 AT_WL_LATE = 34 * KIB
 AT_TABLE0 = 44 * KIB
+AT_FIRST_REF = 52 * KIB
 
 
 def tile_list_cardinality_error_kernel(
@@ -65,7 +66,7 @@ def tile_list_cardinality_error_kernel(
 
         offsets = keep.tile([P, S // 16], U16, name="offsets")
         tab_s = placed([P, 26 * KIB // 4], I32, "tab_s", AT_TABLE_SCALES)[:, 0 : T // 4]
-        w1_c = tile([P, PACK, PASSES, P // 2], I32, "w1_c")
+        w1_c = [tile([P, PACK, P // 2], U32, f"w1_c{a}") for a in range(PASSES)]
         w1_s = tile([P, PACK, PASSES, P // 4], I32, "w1_s")
         v_s = tile([P, S], U8, "v_s")
         v_s1 = tile([P, S // 4], I32, "v_s1")
@@ -74,7 +75,7 @@ def tile_list_cardinality_error_kernel(
         vec_cols = tile([P, PACK + NT], F32, "vec_cols")
 
         zeros_first = placed([P, P], F32, "zeros_first", AT_TABLE0)
-        zeros_second = placed([P, 14 * KIB // 4], I32, "zeros_second", AT_ZEROS_SECOND)[:, 0 : KIB // 4]
+        zeros_second = placed([P, 15 * KIB // 4], I32, "zeros_second", AT_ZEROS_SECOND)[:, 0 : KIB // 4]
         scale_stage = placed([P, PASSES * H // 4], I32, "scale_stage", AT_W1_SCALES)
         w1s_raw = scale_stage[:].rearrange("p (a c) -> p a c", a=PASSES)
 
@@ -100,9 +101,10 @@ def tile_list_cardinality_error_kernel(
             nc.sync.dma_start(
                 w1s_raw[32 * q : 32 * q + PLANE_ROWS, :, :], w1s_rows[PLANE_ROWS * q : PLANE_ROWS * (q + 1)]
             )
-        w1_raw = placed([P, PASSES, H // 2], I32, "w1_raw", AT_W1)
-        nc.sync.dma_start(w1_raw[:], w1_words.bitcast(I32).rearrange("a p c -> p a c"))
+        w1_raw = [placed([P, H // 2], I32, f"w1_raw{a}", AT_W1[a]) for a in range(PASSES)]
+        nc.sync.dma_start(w1_raw[0][:], w1_words.bitcast(I32)[0])
         nc.sync.dma_start(tab_w[1][:], tab_w_rows[1])
+        nc.sync.dma_start(w1_raw[1][:], w1_words.bitcast(I32)[1])
         wl_rows = wl.rearrange("(a p i) n -> a p i n", a=PASSES, i=PACK)
         wl_early = placed([P, PACK, NH], F32, "wl_early", AT_WL_EARLY)
         nc.sync.dma_start(wl_early[:], wl_rows[0][:, :, 0:NH])
@@ -113,14 +115,15 @@ def tile_list_cardinality_error_kernel(
 
         nc.vector.tensor_copy(v_s[:], tab_s.bitcast(U8).indirect(offsets[:]))
         nc.sync.dma_start(v_s1[0:SHIFT_ROWS, :], v_s[PASS_ROWS:P, :].bitcast(I32))
-        nc.vector.tensor_copy(
-            w1_s[:].rearrange("p t a (b w) -> p t (a b) w", w=RUN // 4),
-            w1s_raw.rearrange("p a (b t w) -> p t (a b) w", t=PACK, w=RUN // 4),
+        nc.scalar.copy(
+            w1_s[:].bitcast(U32).rearrange("p t a (b w) -> p t (a b) w", w=RUN // 4),
+            w1s_raw.bitcast(U32).rearrange("p a (b t w) -> p t (a b) w", t=PACK, w=RUN // 4),
         )
-        nc.vector.tensor_copy(
-            w1_c[:].rearrange("p t a (b w) -> p t (a b) w", w=RUN // 2),
-            w1_raw[:].rearrange("p a (b t w) -> p t (a b) w", t=PACK, w=RUN // 2),
-        )
+        for a, copy in enumerate((nc.vector.tensor_copy, nc.scalar.copy)):
+            copy(
+                w1_c[a][:].rearrange("p t (b w) -> p t b w", w=RUN // 2),
+                w1_raw[a][:].bitcast(U32).rearrange("p (b t w) -> p t b w", t=PACK, w=RUN // 2),
+            )
 
         wr_s = placed([P, PASSES, N // 4], I32, "wr_s", AT_WR_SCALES)
         nc.gpsimd.memset(wr_s[:], 0)
@@ -128,7 +131,7 @@ def tile_list_cardinality_error_kernel(
         w2_rows = w2.rearrange("(b t i) n -> t b i n", t=PACK, i=RUN)
         wl_next = placed([P, PACK, NH], F32, "wl_next", AT_WL_NEXT)
         wl_late = [placed([P, PACK, NH], F32, f"wl_late{u}", AT_WL_LATE + 4 * KIB * u) for u in range(2)]
-        nc.sync.dma_start(wl_next[:], wl_rows[0][:, :, NH:N])
+        nc.sync.dma_start(wl_next[:], wl_rows[1][:, :, 0:NH])
         wr_c = placed([P, PASSES, N], I32, "wr_c", AT_WR)
         nc.sync.dma_start(
             wr_c[:], wr_words.rearrange("a p c i -> a p (c i)").bitcast(I32).rearrange("a p c -> p a c")
@@ -140,8 +143,8 @@ def tile_list_cardinality_error_kernel(
             )
         for t in range(PACK):
             nc.sync.dma_start(w2_raw[:, t, :], w2_rows[t])
-        for u in range(2):
-            nc.sync.dma_start(wl_late[u][:], wl_rows[1][:, :, u * NH : (u + 1) * NH])
+        for a in range(PASSES):
+            nc.sync.dma_start(wl_late[a][:], wl_rows[a][:, :, NH:N])
 
         v_c = [
             [tile([P, JW], U32, "v_c00"), placed([P, JW], U32, "v_c01", AT_V01)],
@@ -185,7 +188,7 @@ def tile_list_cardinality_error_kernel(
                 for a in order:
                     nc.tensor.matmul_mx(
                         out=acc[:],
-                        lhsT=w1_c[:, t, a, :].bitcast(U8).bitcast(FP4X4),
+                        lhsT=w1_c[a][:, t, :].bitcast(U8).bitcast(FP4X4),
                         lhsT_scale=w1_s[:, t, a, :].bitcast(U8),
                         rhs=v_c[a][jb][:].bitcast(FP8X4),
                         rhs_scale=v_plane(a, jb),
@@ -198,7 +201,7 @@ def tile_list_cardinality_error_kernel(
                 else:
                     nc.scalar.activation(h_rows[jb][:, t, :], acc[:], ACT.Relu, bias=bias)
 
-        refs, h_q, wl_q, w2_q = {}, {}, {}, {}
+        refs, h_q, wl_q = {}, {}, {}
 
         def reference_tile(c, jb):
             acc = banks[NT * jb + c]
@@ -212,30 +215,37 @@ def tile_list_cardinality_error_kernel(
                     start=(a == 0),
                     stop=(a == PASSES - 1),
                 )
-            ref = tile([P, JW], F32, f"ref{c}{jb}")[:]
-            nc.scalar.activation(ref, acc[:], ACT.Copy, scale=vec_cols[:, PACK + c : PACK + c + 1])
+            if (c, jb) == (0, 0):
+                ref = placed([P, JW], F32, "ref00", AT_FIRST_REF)[:]
+            else:
+                ref = tile([P, JW], F32, f"ref{c}{jb}")[:]
+            gain = vec_cols[:, PACK + c : PACK + c + 1]
+            if (c, jb) == (NT - 1, JB - 1):
+                nc.vector.tensor_scalar(ref, acc[:], gain, None, ALU.mult)
+            else:
+                nc.scalar.activation(ref, acc[:], ACT.Copy, scale=gain)
             refs[(c, jb)] = ref
 
-        def estimate_tile(c, jb):
-            def columns(operand, first):
-                codes, scales = operand
-                return codes[:, first : first + P].bitcast(FP8X4), scales[:, first : first + P]
-
-            passes = (
-                columns(wl_q[0], c * P) + (v_c[0][jb][:], v_plane(0, jb)),
-                columns(w2_q[c // 2], (c % 2) * P) + (h_q[jb][0][:], h_q[jb][1][:]),
-                columns(wl_q[1 + c // 2], (c % 2) * P) + (v_c[1][jb][:], v_plane(1, jb)),
+        def estimate_pass(c, jb, stationary, first, moving, moving_scales, start, stop):
+            codes, scales = stationary
+            nc.tensor.matmul_mx(
+                out=banks[NT * jb + c][:],
+                lhsT=codes[:, first : first + P].bitcast(FP8X4),
+                lhsT_scale=scales[:, first : first + P],
+                rhs=moving.bitcast(FP8X4),
+                rhs_scale=moving_scales,
+                start=start,
+                stop=stop,
             )
-            for n, (codes, scales, moving, moving_scales) in enumerate(passes):
-                nc.tensor.matmul_mx(
-                    out=banks[NT * jb + c][:],
-                    lhsT=codes,
-                    lhsT_scale=scales,
-                    rhs=moving.bitcast(FP8X4),
-                    rhs_scale=moving_scales,
-                    start=(n == 0),
-                    stop=(n == len(passes) - 1),
-                )
+
+        def linear_passes(c, jb, opens):
+            for a in range(PASSES):
+                first = a * NH + (c % 2) * P
+                start, stop = opens and a == 0, not opens and a == PASSES - 1
+                estimate_pass(c, jb, wl_q[c // 2], first, v_c[a][jb][:], v_plane(a, jb), start, stop)
+
+        def branch_pass(c, jb, opens):
+            estimate_pass(c, jb, w2_q, c * P, h_q[jb][0][:], h_q[jb][1][:], opens, not opens)
 
         def finish_tile(c, jb, pieces=1):
             acc = banks[NT * jb + c]
@@ -250,43 +260,47 @@ def tile_list_cardinality_error_kernel(
 
         on_vector, on_scalar = nc.vector.tensor_copy, nc.scalar.copy
 
-        wl0 = tile([P, PACK * N], BF16, "wl0")
+        wl_first = tile([P, PACK * N], BF16, "wl_first")
         nc.gpsimd.tensor_scalar(
-            wl0[:, 0 : PACK * NH].rearrange("p (c t) -> p c t", t=PACK),
+            wl_first[:, 0 : PACK * NH].rearrange("p (c t) -> p c t", t=PACK),
             wl_early[:].rearrange("p t c -> p c t"),
             1.0,
             0.0,
             ALU.mult,
             ALU.add,
         )
-        interleave(on_vector, wl0[:, PACK * NH : PACK * N], wl_next[:])
-        h_first = grouped(on_vector, h_rows[0][:], "h_first", AT_WL_NEXT)
-        wl_q[0] = quantize(wl0, "wl0")
+        interleave(on_vector, wl_first[:, PACK * NH : PACK * N], wl_next[:])
+        h_first = grouped(on_vector, h_rows[0][:], "h_first")
+        wl_q[0] = quantize(wl_first, "wl_first")
         h_q[0] = quantize(h_first, "h_first")
-        w2_first = grouped(on_vector, w2_raw[:, :, 0:NH], "w2_first")
         h_second = grouped(on_vector, h_rows[1][:], "h_second")
-        wl10 = grouped(on_vector, wl_late[0][:], "wl10")
-        w2_q[0] = quantize(w2_first, "w2_first", AT_WL_LATE)
-        h_q[1] = quantize(h_second, "h_second", AT_WL_LATE + KIB)
-        wl_q[1] = quantize(wl10, "wl10")
+        w2_grouped = grouped(on_vector, w2_raw[:], "w2_grouped")
+        h_q[1] = quantize(h_second, "h_second")
+        w2_q = quantize(w2_grouped, "w2")
         for c in range(NT):
             reference_tile(c, 0)
-        w2_second = grouped(on_scalar, w2_raw[:, :, NH:N], "w2_second")
         for c in (0, 1):
             reference_tile(c, 1)
-        wl11 = grouped(on_scalar, wl_late[1][:], "wl11")
+        wl_second = tile([P, PACK * N], BF16, "wl_second")
+        for a in range(PASSES):
+            interleave(on_scalar, wl_second[:, a * PACK * NH : (a + 1) * PACK * NH], wl_late[a][:])
         for c in (2, 3):
             reference_tile(c, 1)
-        for jb in range(JB):
-            for c in (0, 1):
-                estimate_tile(c, jb)
-        w2_q[1] = quantize(w2_second, "w2_second")
+        linear_passes(0, 0, True)
+        linear_passes(1, 0, True)
+        linear_passes(0, 1, True)
+        branch_pass(0, 0, False)
+        branch_pass(1, 0, False)
+        linear_passes(1, 1, True)
+        branch_pass(0, 1, False)
+        branch_pass(1, 1, False)
         finish_tile(0, 0)
         finish_tile(1, 0)
-        wl_q[2] = quantize(wl11, "wl11")
+        wl_q[1] = quantize(wl_second, "wl_second", AT_FIRST_REF)
         finish_tile(0, 1)
         finish_tile(1, 1)
-        second_half = ((2, 0), (3, 0), (2, 1), (3, 1))
-        for c, jb in second_half:
-            estimate_tile(c, jb)
-            finish_tile(c, jb, 2 if jb == 1 else 1)
+        for jb in range(JB):
+            for c in (2, 3):
+                branch_pass(c, jb, True)
+                linear_passes(c, jb, False)
+                finish_tile(c, jb, 2 if jb == 1 else 1)

@@ -31,22 +31,21 @@ SHIFT_ROWS = P - PASS_ROWS
 RUN = 8
 BANKS = 8
 KIB = 1024
-EARLY_SUMS = 4
+EARLY_SUMS = 6
 
 AT_ZEROS_SECOND = 0
-AT_WL_EARLY = 0
 AT_TABLE1 = 4 * KIB
 AT_W1 = (12 * KIB, 14 * KIB)
 AT_V01 = 12 * KIB
 AT_W1_SCALES = 15 * KIB
 AT_TABLE_SCALES = 16 * KIB
-AT_WR_SCALES = 17 * KIB
 AT_WL_NEXT = 18 * KIB
 AT_WR = 22 * KIB
 AT_W2 = 26 * KIB
 AT_WL_LATE = 34 * KIB
-AT_TABLE0 = 44 * KIB
-AT_FIRST_REF = 52 * KIB
+AT_WL_EARLY = 42 * KIB
+AT_TABLE0 = 46 * KIB
+AT_FIRST_REF = 54 * KIB
 
 
 def tile_list_cardinality_error_kernel(
@@ -65,7 +64,7 @@ def tile_list_cardinality_error_kernel(
             return shared.tile(shape, dtype, name=name, align_bytes=64, offset=offset)
 
         offsets = keep.tile([P, S // 16], U16, name="offsets")
-        tab_s = placed([P, 26 * KIB // 4], I32, "tab_s", AT_TABLE_SCALES)[:, 0 : T // 4]
+        tab_s = placed([P, 30 * KIB // 4], I32, "tab_s", AT_TABLE_SCALES)[:, 0 : T // 4]
         w1_c = [tile([P, PACK, P // 2], U32, f"w1_c{a}") for a in range(PASSES)]
         w1_s = tile([P, PACK, PASSES, P // 4], I32, "w1_s")
         v_s = tile([P, S], U8, "v_s")
@@ -85,6 +84,8 @@ def tile_list_cardinality_error_kernel(
         nc.vector.memset(zeros_second, 0)
         nc.vector.tensor_copy(scale_stage[:], zeros_second)
         nc.vector.memset(v_s1[:], 0)
+        wr_s = tile([P, PASSES, N // 4], I32, "wr_s")
+        nc.vector.memset(wr_s[:], 0)
         make_identity(nc, ident[:])
 
         nc.sync.dma_start(offsets[:], offs)
@@ -105,9 +106,12 @@ def tile_list_cardinality_error_kernel(
         nc.sync.dma_start(w1_raw[0][:], w1_words.bitcast(I32)[0])
         nc.sync.dma_start(tab_w[1][:], tab_w_rows[1])
         nc.sync.dma_start(w1_raw[1][:], w1_words.bitcast(I32)[1])
+        wrs_rows = wr_scales.bitcast(I32).rearrange("a q c -> q a c")
+        for q in range(QUADS):
+            nc.sync.dma_start(
+                wr_s[32 * q : 32 * q + PLANE_ROWS, :, :], wrs_rows[PLANE_ROWS * q : PLANE_ROWS * (q + 1)]
+            )
         wl_rows = wl.rearrange("(a p i) n -> a p i n", a=PASSES, i=PACK)
-        wl_early = placed([P, PACK, NH], F32, "wl_early", AT_WL_EARLY)
-        nc.sync.dma_start(wl_early[:], wl_rows[0][:, :, 0:NH])
 
         banks = [psum.tile([P, JW], F32, name=f"bank{b}") for b in range(BANKS)]
         nc.tensor.transpose(banks[-1][:, 0:P], vec_rows[:], ident[:])
@@ -125,22 +129,17 @@ def tile_list_cardinality_error_kernel(
                 w1_raw[a][:].bitcast(U32).rearrange("p (b t w) -> p t b w", t=PACK, w=RUN // 2),
             )
 
-        wr_s = placed([P, PASSES, N // 4], I32, "wr_s", AT_WR_SCALES)
-        nc.gpsimd.memset(wr_s[:], 0)
         w2_raw = placed([P, PACK, N], F32, "w2_raw", AT_W2)
         w2_rows = w2.rearrange("(b t i) n -> t b i n", t=PACK, i=RUN)
         wl_next = placed([P, PACK, NH], F32, "wl_next", AT_WL_NEXT)
         wl_late = [placed([P, PACK, NH], F32, f"wl_late{u}", AT_WL_LATE + 4 * KIB * u) for u in range(2)]
-        nc.sync.dma_start(wl_next[:], wl_rows[1][:, :, 0:NH])
+        wl_early = placed([P, PACK, NH], F32, "wl_early", AT_WL_EARLY)
+        nc.sync.dma_start(wl_early[:], wl_rows[0][:, :, 0:NH])
         wr_c = placed([P, PASSES, N], I32, "wr_c", AT_WR)
         nc.sync.dma_start(
             wr_c[:], wr_words.rearrange("a p c i -> a p (c i)").bitcast(I32).rearrange("a p c -> p a c")
         )
-        wrs_rows = wr_scales.bitcast(I32).rearrange("a q c -> q a c")
-        for q in range(QUADS):
-            nc.sync.dma_start(
-                wr_s[32 * q : 32 * q + PLANE_ROWS, :, :], wrs_rows[PLANE_ROWS * q : PLANE_ROWS * (q + 1)]
-            )
+        nc.sync.dma_start(wl_next[:], wl_rows[1][:, :, 0:NH])
         for t in range(PACK):
             nc.sync.dma_start(w2_raw[:, t, :], w2_rows[t])
         for a in range(PASSES):
@@ -269,10 +268,10 @@ def tile_list_cardinality_error_kernel(
             ALU.mult,
             ALU.add,
         )
-        interleave(on_vector, wl_first[:, PACK * NH : PACK * N], wl_next[:])
         h_first = grouped(on_vector, h_rows[0][:], "h_first")
-        wl_q[0] = quantize(wl_first, "wl_first")
+        interleave(on_vector, wl_first[:, PACK * NH : PACK * N], wl_next[:])
         h_q[0] = quantize(h_first, "h_first")
+        wl_q[0] = quantize(wl_first, "wl_first")
         h_second = grouped(on_vector, h_rows[1][:], "h_second")
         w2_grouped = grouped(on_vector, w2_raw[:], "w2_grouped")
         h_q[1] = quantize(h_second, "h_second")

@@ -31,6 +31,7 @@ SHIFT_ROWS = P - PASS_ROWS
 RUN = 8
 BANKS = 8
 KIB = 1024
+WARM_UP = 3
 EARLY_SUMS = 6
 
 AT_ZEROS_SECOND = 0
@@ -159,6 +160,17 @@ def tile_list_cardinality_error_kernel(
 
         def v_plane(a, jb):
             return (v_s[:], v_s1[:].bitcast(U8))[a][:, jb * JW : (jb + 1) * JW]
+
+        for n in range(WARM_UP):
+            nc.tensor.matmul_mx(
+                out=banks[0][:],
+                lhsT=tab_w[0][:, 0:P].bitcast(FP8X4),
+                lhsT_scale=v_s[:, 0:P],
+                rhs=tab_w[0][:, 0:JW].bitcast(FP8X4),
+                rhs_scale=v_s[:, 0:JW],
+                start=True,
+                stop=True,
+            )
 
         def interleave(copy, dst, src):
             copy(

@@ -28,7 +28,6 @@ QUADS = 4
 PLANE_ROWS = 4
 PASS_ROWS = 16
 SHIFT_ROWS = P - PASS_ROWS
-RUN = 8
 BANKS = 8
 KIB = 1024
 WARM_UP = 3
@@ -36,8 +35,9 @@ EARLY_SUMS = 6
 
 AT_ZEROS_SECOND = 0
 AT_TABLE1 = 4 * KIB
-AT_W1 = (12 * KIB, 14 * KIB)
-AT_V01 = 12 * KIB
+AT_W1 = (12 * KIB, 0)
+AT_W1_PLANE1 = 12 * KIB
+AT_V01 = 12 * KIB + KIB // 2
 AT_W1_SCALES = 15 * KIB
 AT_TABLE_SCALES = 16 * KIB
 AT_WL_NEXT = 18 * KIB
@@ -66,13 +66,13 @@ def tile_list_cardinality_error_kernel(
 
         offsets = keep.tile([P, S // 16], U16, name="offsets")
         tab_s = placed([P, 30 * KIB // 4], I32, "tab_s", AT_TABLE_SCALES)[:, 0 : T // 4]
-        w1_c = [tile([P, PACK, P // 2], U32, f"w1_c{a}") for a in range(PASSES)]
-        w1_s = tile([P, PACK, PASSES, P // 4], I32, "w1_s")
+        w1_c = [tile([P, PACK, P], U16, f"w1_c{a}") for a in range(PASSES)]
+        w1_s = [tile([P, PACK, P], U8, "w1_s0"), placed([P, PACK, P], U8, "w1_s1", AT_W1_PLANE1)]
         v_s = tile([P, S], U8, "v_s")
         v_s1 = tile([P, S // 4], I32, "v_s1")
         vec_rows = tile([P, P], F32, "vec_rows")
         ident = tile([P, P], F32, "ident")
-        vec_cols = tile([P, PACK + NT], F32, "vec_cols")
+        vec_cols = tile([P, NT], F32, "vec_cols")
 
         zeros_first = placed([P, P], F32, "zeros_first", AT_TABLE0)
         zeros_second = placed([P, 15 * KIB // 4], I32, "zeros_second", AT_ZEROS_SECOND)[:, 0 : KIB // 4]
@@ -93,8 +93,9 @@ def tile_list_cardinality_error_kernel(
         tab_s_rows = tab_scales.bitcast(I32).rearrange("a (q r) c -> r q a c", r=PLANE_ROWS)
         for r in range(PLANE_ROWS):
             nc.sync.dma_start(tab_s[r:P:PASS_ROWS, :], tab_s_rows[r])
-        nc.sync.dma_start(vec_rows[0:PACK, :], b1.rearrange("(b t i) -> t b i", t=PACK, i=RUN))
-        nc.sync.dma_start(vec_rows[PACK : PACK + NT, :], gr.rearrange("(c p) -> c p", p=P))
+        bias = tile([P, PACK], F32, "bias")
+        nc.sync.dma_start(bias[:], b1.rearrange("(p t) -> p t", t=PACK))
+        nc.sync.dma_start(vec_rows[0:NT, :], gr.rearrange("(c p) -> c p", p=P))
         tab_w_rows = tab_words.rearrange("a p t i -> a p (t i)").bitcast(I32)
         tab_w = [placed([P, T], I32, "tab_w0", AT_TABLE0), placed([P, T], I32, "tab_w1", AT_TABLE1)]
         nc.sync.dma_start(tab_w[0][:], tab_w_rows[0])
@@ -116,22 +117,15 @@ def tile_list_cardinality_error_kernel(
 
         banks = [psum.tile([P, JW], F32, name=f"bank{b}") for b in range(BANKS)]
         nc.tensor.transpose(banks[-1][:, 0:P], vec_rows[:], ident[:])
-        nc.scalar.copy(vec_cols[:], banks[-1][:, 0 : PACK + NT])
+        nc.scalar.copy(vec_cols[:], banks[-1][:, 0:NT])
 
         nc.vector.tensor_copy(v_s[:], tab_s.bitcast(U8).indirect(offsets[:]))
         nc.sync.dma_start(v_s1[0:SHIFT_ROWS, :], v_s[PASS_ROWS:P, :].bitcast(I32))
-        nc.scalar.copy(
-            w1_s[:].bitcast(U32).rearrange("p t a (b w) -> p t (a b) w", w=RUN // 4),
-            w1s_raw.bitcast(U32).rearrange("p a (b t w) -> p t (a b) w", t=PACK, w=RUN // 4),
-        )
-        for a, copy in enumerate((nc.vector.tensor_copy, nc.scalar.copy)):
-            copy(
-                w1_c[a][:].rearrange("p t (b w) -> p t b w", w=RUN // 2),
-                w1_raw[a][:].bitcast(U32).rearrange("p (b t w) -> p t b w", t=PACK, w=RUN // 2),
-            )
+        for a, copy in enumerate((nc.vector.tensor_copy, nc.gpsimd.tensor_copy)):
+            nc.scalar.copy(w1_c[a][:], w1_raw[a][:].bitcast(U16).rearrange("p (m t) -> p t m", t=PACK))
+            copy(w1_s[a][:], w1s_raw[:, a, :].bitcast(U8).rearrange("p (m t) -> p t m", t=PACK))
 
         w2_raw = placed([P, PACK, N], F32, "w2_raw", AT_W2)
-        w2_rows = w2.rearrange("(b t i) n -> t b i n", t=PACK, i=RUN)
         wl_next = placed([P, PACK, NH], F32, "wl_next", AT_WL_NEXT)
         wl_late = [placed([P, PACK, NH], F32, f"wl_late{u}", AT_WL_LATE + 4 * KIB * u) for u in range(2)]
         wl_early = placed([P, PACK, NH], F32, "wl_early", AT_WL_EARLY)
@@ -141,8 +135,7 @@ def tile_list_cardinality_error_kernel(
             wr_c[:], wr_words.rearrange("a p c i -> a p (c i)").bitcast(I32).rearrange("a p c -> p a c")
         )
         nc.sync.dma_start(wl_next[:], wl_rows[1][:, :, 0:NH])
-        for t in range(PACK):
-            nc.sync.dma_start(w2_raw[:, t, :], w2_rows[t])
+        nc.sync.dma_start(w2_raw[:], w2.rearrange("(p t) n -> p t n", t=PACK))
         for a in range(PASSES):
             nc.sync.dma_start(wl_late[a][:], wl_rows[a][:, :, NH:N])
 
@@ -200,17 +193,16 @@ def tile_list_cardinality_error_kernel(
                     nc.tensor.matmul_mx(
                         out=acc[:],
                         lhsT=w1_c[a][:, t, :].bitcast(U8).bitcast(FP4X4),
-                        lhsT_scale=w1_s[:, t, a, :].bitcast(U8),
+                        lhsT_scale=w1_s[a][:, t, :],
                         rhs=v_c[a][jb][:].bitcast(FP8X4),
                         rhs_scale=v_plane(a, jb),
                         start=(a == order[0]),
                         stop=(a == order[-1]),
                     )
-                bias = vec_cols[:, t : t + 1]
                 if (jb, t) == (0, PACK - 1):
-                    nc.vector.tensor_scalar(h_rows[jb][:, t, :], acc[:], bias, 0.0, ALU.add, ALU.max)
+                    nc.vector.tensor_scalar(h_rows[jb][:, t, :], acc[:], bias[:, t : t + 1], 0.0, ALU.add, ALU.max)
                 else:
-                    nc.scalar.activation(h_rows[jb][:, t, :], acc[:], ACT.Relu, bias=bias)
+                    nc.scalar.activation(h_rows[jb][:, t, :], acc[:], ACT.Relu, bias=bias[:, t : t + 1])
 
         refs, h_q, wl_q = {}, {}, {}
 
@@ -230,7 +222,7 @@ def tile_list_cardinality_error_kernel(
                 ref = placed([P, JW], F32, "ref00", AT_FIRST_REF)[:]
             else:
                 ref = tile([P, JW], F32, f"ref{c}{jb}")[:]
-            gain = vec_cols[:, PACK + c : PACK + c + 1]
+            gain = vec_cols[:, c : c + 1]
             if (c, jb) == (NT - 1, JB - 1):
                 nc.vector.tensor_scalar(ref, acc[:], gain, None, ALU.mult)
             else:

@@ -31,7 +31,8 @@ SHIFT_ROWS = P - PASS_ROWS
 BANKS = 8
 KIB = 1024
 WARM_UP = 3
-EARLY_SUMS = 6
+EARLY_SUMS = 1
+HALF = JW // 2
 
 AT_ZEROS_SECOND = 0
 AT_TABLE1 = 4 * KIB
@@ -143,13 +144,19 @@ def tile_list_cardinality_error_kernel(
             [tile([P, JW], U32, "v_c00"), placed([P, JW], U32, "v_c01", AT_V01)],
             [tile([P, JW], U32, "v_c10"), tile([P, JW], U32, "v_c11")],
         ]
-        list_cols = JW // 16
-        for a in range(PASSES):
-            for jb in range(JB):
-                nc.vector.tensor_copy(
-                    v_c[a][jb][:],
-                    tab_w[a][:].bitcast(U32).indirect(offsets[:, jb * list_cols : (jb + 1) * list_cols]),
-                )
+
+        def gather_words(a, jb, first, width):
+            column = (jb * JW + first) // 16
+            nc.vector.tensor_copy(
+                v_c[a][jb][:, first : first + width],
+                tab_w[a][:].bitcast(U32).indirect(offsets[:, column : column + width // 16]),
+            )
+
+        gather_words(0, 0, 0, JW)
+        gather_words(0, 1, 0, JW)
+        gather_words(1, 0, 0, HALF)
+        gather_words(1, 0, HALF, HALF)
+        gather_words(1, 1, 0, JW)
 
         def v_plane(a, jb):
             return (v_s[:], v_s1[:].bitcast(U8))[a][:, jb * JW : (jb + 1) * JW]
@@ -185,24 +192,45 @@ def tile_list_cardinality_error_kernel(
             return codes, scales
 
         h_rows = [tile([P, PACK, JW], BF16, f"h_rows{jb}") for jb in range(JB)]
-        for jb in range(JB):
+
+        def hidden_pass(acc, t, jb, a, first, width, start, stop):
+            nc.tensor.matmul_mx(
+                out=acc,
+                lhsT=w1_c[a][:, t, :].bitcast(U8).bitcast(FP4X4),
+                lhsT_scale=w1_s[a][:, t, :],
+                rhs=v_c[a][jb][:, first : first + width].bitcast(FP8X4),
+                rhs_scale=v_plane(a, jb)[:, first : first + width],
+                start=start,
+                stop=stop,
+            )
+
+        def relu(acc, t, jb, first, width, by_vector):
+            dst = h_rows[jb][:, t, first : first + width]
+            if by_vector:
+                nc.vector.tensor_scalar(dst, acc, bias[:, t : t + 1], 0.0, ALU.add, ALU.max)
+            else:
+                nc.scalar.activation(dst, acc, ACT.Relu, bias=bias[:, t : t + 1])
+
+        def half_sum(half, t):
+            return banks[2 * half + t // 2][:, (t % 2) * HALF : (t % 2 + 1) * HALF]
+
+        for half in range(2):
             for t in range(PACK):
-                acc = banks[PACK * jb + t]
-                order = (1, 0) if PACK * jb + t >= EARLY_SUMS else (0, 1)
-                for a in order:
-                    nc.tensor.matmul_mx(
-                        out=acc[:],
-                        lhsT=w1_c[a][:, t, :].bitcast(U8).bitcast(FP4X4),
-                        lhsT_scale=w1_s[a][:, t, :],
-                        rhs=v_c[a][jb][:].bitcast(FP8X4),
-                        rhs_scale=v_plane(a, jb),
-                        start=(a == order[0]),
-                        stop=(a == order[-1]),
-                    )
-                if (jb, t) == (0, PACK - 1):
-                    nc.vector.tensor_scalar(h_rows[jb][:, t, :], acc[:], bias[:, t : t + 1], 0.0, ALU.add, ALU.max)
-                else:
-                    nc.scalar.activation(h_rows[jb][:, t, :], acc[:], ACT.Relu, bias=bias[:, t : t + 1])
+                hidden_pass(half_sum(half, t), t, 0, 0, half * HALF, HALF, t % 2 == 0, False)
+        for t in range(EARLY_SUMS):
+            hidden_pass(banks[PACK + t][:], t, 1, 0, 0, JW, True, False)
+        for half in range(2):
+            for pair in range(2):
+                for t in (2 * pair, 2 * pair + 1):
+                    hidden_pass(half_sum(half, t), t, 0, 1, half * HALF, HALF, False, t % 2 == 1)
+                for t in (2 * pair, 2 * pair + 1):
+                    relu(half_sum(half, t), t, 0, half * HALF, HALF, (half, pair) == (1, 1))
+        for t in range(PACK):
+            early = t < EARLY_SUMS
+            hidden_pass(banks[PACK + t][:], t, 1, 1, 0, JW, not early, early)
+            if not early:
+                hidden_pass(banks[PACK + t][:], t, 1, 0, 0, JW, False, True)
+            relu(banks[PACK + t][:], t, 1, 0, JW, False)
 
         refs, h_q, wl_q = {}, {}, {}
 
@@ -250,13 +278,12 @@ def tile_list_cardinality_error_kernel(
         def branch_pass(c, jb, opens):
             estimate_pass(c, jb, w2_q, c * P, h_q[jb][0][:], h_q[jb][1][:], opens, not opens)
 
-        def finish_tile(c, jb, pieces=1):
+        def finish_tile(c, jb, widths=(JW,)):
             acc = banks[NT * jb + c]
             diff = tile([P, JW], F32, f"diff{c}{jb}")
             err = tile([P, JW], F32, f"err{c}{jb}")
-            width = JW // pieces
-            for piece in range(pieces):
-                cols = slice(piece * width, (piece + 1) * width)
+            for piece, width in enumerate(widths):
+                cols = slice(sum(widths[:piece]), sum(widths[:piece]) + width)
                 nc.vector.tensor_tensor(diff[:, cols], acc[:, cols], refs[(c, jb)][:, cols], ALU.subtract)
                 nc.scalar.activation(err[:, cols], diff[:, cols], ACT.Abs)
                 nc.sync.dma_start(out[c * P : (c + 1) * P, jb * JW : (jb + 1) * JW][:, cols], err[:, cols])
@@ -306,4 +333,4 @@ def tile_list_cardinality_error_kernel(
             for c in (2, 3):
                 branch_pass(c, jb, True)
                 linear_passes(c, jb, False)
-                finish_tile(c, jb, 2 if jb == 1 else 1)
+                finish_tile(c, jb, ((JW,), (JW,), (HALF, HALF), (HALF, P, P))[2 * jb + c - 2])

@@ -31,8 +31,8 @@ SHIFT_ROWS = P - PASS_ROWS
 BANKS = 8
 KIB = 1024
 WARM_UP = 3
-EARLY_SUMS = 1
 HALF = JW // 2
+LAST_ON_VECTOR = 48
 
 AT_ZEROS_SECOND = 0
 AT_TABLE1 = 4 * KIB
@@ -211,25 +211,30 @@ def tile_list_cardinality_error_kernel(
             else:
                 nc.scalar.activation(dst, acc, ACT.Relu, bias=bias[:, t : t + 1])
 
-        def half_sum(half, t):
-            return banks[2 * half + t // 2][:, (t % 2) * HALF : (t % 2 + 1) * HALF]
+        first_banks = [banks[5], banks[6], banks[7], banks[0]]
 
-        for half in range(2):
-            for t in range(PACK):
-                hidden_pass(half_sum(half, t), t, 0, 0, half * HALF, HALF, t % 2 == 0, False)
-        for t in range(EARLY_SUMS):
-            hidden_pass(banks[PACK + t][:], t, 1, 0, 0, JW, True, False)
-        for half in range(2):
-            for pair in range(2):
-                for t in (2 * pair, 2 * pair + 1):
-                    hidden_pass(half_sum(half, t), t, 0, 1, half * HALF, HALF, False, t % 2 == 1)
-                for t in (2 * pair, 2 * pair + 1):
-                    relu(half_sum(half, t), t, 0, half * HALF, HALF, (half, pair) == (1, 1))
+        def second_sum(t):
+            return banks[2 + t // 2][:, (t % 2) * HALF : (t % 2 + 1) * HALF]
+
         for t in range(PACK):
-            early = t < EARLY_SUMS
-            hidden_pass(banks[PACK + t][:], t, 1, 1, 0, JW, not early, early)
-            if not early:
-                hidden_pass(banks[PACK + t][:], t, 1, 0, 0, JW, False, True)
+            hidden_pass(first_banks[t][:, 0:HALF], t, 0, 0, 0, HALF, True, False)
+        for t in range(PACK):
+            hidden_pass(second_sum(t), t, 0, 0, HALF, HALF, t % 2 == 0, False)
+        hidden_pass(banks[PACK][:], 0, 1, 0, 0, JW, True, False)
+        for t in range(PACK):
+            hidden_pass(first_banks[t][:, 0:HALF], t, 0, 1, 0, HALF, False, True)
+            relu(first_banks[t][:, 0:HALF], t, 0, 0, HALF, False)
+        for pair in range(2):
+            for t in (2 * pair, 2 * pair + 1):
+                hidden_pass(second_sum(t), t, 0, 1, HALF, HALF, False, t % 2 == 1)
+            for t in (2 * pair, 2 * pair + 1):
+                relu(second_sum(t), t, 0, HALF, HALF, pair == 1)
+        for t in (1, 2):
+            hidden_pass(banks[PACK + t][:], t, 1, 0, 0, JW, True, False)
+        for t in range(PACK):
+            if t == PACK - 1:
+                hidden_pass(banks[PACK + t][:], t, 1, 0, 0, JW, True, False)
+            hidden_pass(banks[PACK + t][:], t, 1, 1, 0, JW, False, True)
             relu(banks[PACK + t][:], t, 1, 0, JW, False)
 
         refs, h_q, wl_q = {}, {}, {}
@@ -257,34 +262,38 @@ def tile_list_cardinality_error_kernel(
                 nc.scalar.activation(ref, acc[:], ACT.Copy, scale=gain)
             refs[(c, jb)] = ref
 
-        def estimate_pass(c, jb, stationary, first, moving, moving_scales, start, stop):
+        def estimate_sum(c, jb, cols):
+            if (c, jb) == (NT - 1, JB - 1) and cols.start >= HALF:
+                return banks[0][:, cols]
+            return banks[NT * jb + c][:, cols]
+
+        def estimate_pass(c, jb, cols, stationary, first, moving, moving_scales, start, stop):
             codes, scales = stationary
             nc.tensor.matmul_mx(
-                out=banks[NT * jb + c][:],
+                out=estimate_sum(c, jb, cols),
                 lhsT=codes[:, first : first + P].bitcast(FP8X4),
                 lhsT_scale=scales[:, first : first + P],
-                rhs=moving.bitcast(FP8X4),
-                rhs_scale=moving_scales,
+                rhs=moving[:, cols].bitcast(FP8X4),
+                rhs_scale=moving_scales[:, cols],
                 start=start,
                 stop=stop,
             )
 
-        def linear_passes(c, jb, opens):
+        def linear_passes(c, jb, opens, cols=slice(0, JW)):
             for a in range(PASSES):
                 first = a * NH + (c % 2) * P
                 start, stop = opens and a == 0, not opens and a == PASSES - 1
-                estimate_pass(c, jb, wl_q[c // 2], first, v_c[a][jb][:], v_plane(a, jb), start, stop)
+                estimate_pass(c, jb, cols, wl_q[c // 2], first, v_c[a][jb][:], v_plane(a, jb), start, stop)
 
-        def branch_pass(c, jb, opens):
-            estimate_pass(c, jb, w2_q, c * P, h_q[jb][0][:], h_q[jb][1][:], opens, not opens)
+        def branch_pass(c, jb, opens, cols=slice(0, JW)):
+            estimate_pass(c, jb, cols, w2_q, c * P, h_q[jb][0][:], h_q[jb][1][:], opens, not opens)
 
         def finish_tile(c, jb, widths=(JW,)):
-            acc = banks[NT * jb + c]
             diff = tile([P, JW], F32, f"diff{c}{jb}")
             err = tile([P, JW], F32, f"err{c}{jb}")
             for piece, width in enumerate(widths):
                 cols = slice(sum(widths[:piece]), sum(widths[:piece]) + width)
-                nc.vector.tensor_tensor(diff[:, cols], acc[:, cols], refs[(c, jb)][:, cols], ALU.subtract)
+                nc.vector.tensor_tensor(diff[:, cols], estimate_sum(c, jb, cols), refs[(c, jb)][:, cols], ALU.subtract)
                 nc.scalar.activation(err[:, cols], diff[:, cols], ACT.Abs)
                 nc.sync.dma_start(out[c * P : (c + 1) * P, jb * JW : (jb + 1) * JW][:, cols], err[:, cols])
 
@@ -299,7 +308,13 @@ def tile_list_cardinality_error_kernel(
             ALU.mult,
             ALU.add,
         )
-        h_first = grouped(on_vector, h_rows[0][:], "h_first")
+        h_first = tile([P, PACK * JW], BF16, "h_first")
+        for half in range(2):
+            interleave(
+                on_vector,
+                h_first[:, half * PACK * HALF : (half + 1) * PACK * HALF],
+                h_rows[0][:, :, half * HALF : (half + 1) * HALF],
+            )
         interleave(on_vector, wl_first[:, PACK * NH : PACK * N], wl_next[:])
         h_q[0] = quantize(h_first, "h_first")
         wl_q[0] = quantize(wl_first, "wl_first")
@@ -312,25 +327,28 @@ def tile_list_cardinality_error_kernel(
         for c in (0, 1):
             reference_tile(c, 1)
         wl_second = tile([P, PACK * N], BF16, "wl_second")
-        for a in range(PASSES):
-            interleave(on_scalar, wl_second[:, a * PACK * NH : (a + 1) * PACK * NH], wl_late[a][:])
+        interleave(on_scalar, wl_second[:, 0 : PACK * NH], wl_late[0][:])
+        split = NH - LAST_ON_VECTOR
+        interleave(on_scalar, wl_second[:, PACK * NH : PACK * (NH + split)], wl_late[1][:, :, 0:split])
         for c in (2, 3):
             reference_tile(c, 1)
+        interleave(on_vector, wl_second[:, PACK * (NH + split) :], wl_late[1][:, :, split:NH])
         linear_passes(0, 0, True)
         linear_passes(1, 0, True)
-        linear_passes(0, 1, True)
         branch_pass(0, 0, False)
         branch_pass(1, 0, False)
-        linear_passes(1, 1, True)
-        branch_pass(0, 1, False)
-        branch_pass(1, 1, False)
+        for c in (0, 1):
+            linear_passes(c, 1, True)
+            branch_pass(c, 1, False)
         finish_tile(0, 0)
-        finish_tile(1, 0)
         wl_q[1] = quantize(wl_second, "wl_second", AT_FIRST_REF)
+        finish_tile(1, 0)
         finish_tile(0, 1)
         finish_tile(1, 1)
         for jb in range(JB):
             for c in (2, 3):
-                branch_pass(c, jb, True)
-                linear_passes(c, jb, False)
+                last = (c, jb) == (NT - 1, JB - 1)
+                for cols in (slice(0, HALF), slice(HALF, JW)) if last else (slice(0, JW),):
+                    branch_pass(c, jb, True, cols)
+                    linear_passes(c, jb, False, cols)
                 finish_tile(c, jb, ((JW,), (JW,), (HALF, HALF), (HALF, P, P))[2 * jb + c - 2])

@@ -60,10 +60,10 @@ def tile_list_cardinality_error_kernel(
         psum = ctx.enter_context(tc.psum_pool(name="psum", bufs=1))
 
         def tile(shape, dtype, name):
-            return keep.tile(shape, dtype, name=name, align_bytes=64)
+            return keep.tile(shape, dtype, name=name, align_bytes=256)
 
         def placed(shape, dtype, name, offset):
-            return shared.tile(shape, dtype, name=name, align_bytes=64, offset=offset)
+            return shared.tile(shape, dtype, name=name, align_bytes=256, offset=offset)
 
         offsets = keep.tile([P, S // 16], U16, name="offsets")
         tab_s = placed([P, 30 * KIB // 4], I32, "tab_s", AT_TABLE_SCALES)[:, 0 : T // 4]

from contextlib import ExitStack

import concourse.mybir as mybir
from concourse.masks import make_identity

K, H, N, T, S = 1024, 512, 512, 2048, 1024
FLOPS = 2 * S * (K * H + H * N + 2 * K * N)

F32 = mybir.dt.float32
BF16 = mybir.dt.bfloat16
I32 = mybir.dt.int32
U32 = mybir.dt.uint32
U16 = mybir.dt.uint16
U8 = mybir.dt.uint8
FP8X4 = mybir.dt.float8_e4m3fn_x4
FP4X4 = mybir.dt.float4_e2m1fn_x4
ACT = mybir.ActivationFunctionType
ALU = mybir.AluOpType

P = 128
PACK = 4
PASSES = K // (P * PACK)
JW = 512
JB = S // JW
NT = N // P
NH = N // 2
QUADS = 4
PLANE_ROWS = 4
PASS_ROWS = 16
SHIFT_ROWS = P - PASS_ROWS
BANKS = 8
KIB = 1024
WARM_UP = 3
HALF = JW // 2
LAST_ON_VECTOR = 48

AT_ZEROS_SECOND = 0
AT_TABLE1 = 4 * KIB
AT_W1 = (12 * KIB, 0)
AT_W1_PLANE1 = 12 * KIB
AT_V01 = 12 * KIB + KIB // 2
AT_W1_SCALES = 15 * KIB
AT_TABLE_SCALES = 16 * KIB
AT_WL_NEXT = 18 * KIB
AT_WR = 22 * KIB
AT_W2 = 26 * KIB
AT_WL_LATE = 34 * KIB
AT_WL_EARLY = 42 * KIB
AT_TABLE0 = 46 * KIB
AT_FIRST_REF = 54 * KIB


def tile_list_cardinality_error_kernel(
    tc, tab_words, tab_scales, offs, w1_words, w1_scales, b1, w2, wl, wr_words, wr_scales, gr, out
):
    nc = tc.nc
    with ExitStack() as ctx:
        keep = ctx.enter_context(tc.tile_pool(name="keep", bufs=1))
        shared = ctx.enter_context(tc.tile_pool(name="shared", bufs=1))
        psum = ctx.enter_context(tc.psum_pool(name="psum", bufs=1))

        def tile(shape, dtype, name):
            return keep.tile(shape, dtype, name=name, align_bytes=256)

        def placed(shape, dtype, name, offset):
            return shared.tile(shape, dtype, name=name, align_bytes=256, offset=offset)

        offsets = keep.tile([P, S // 16], U16, name="offsets")
        tab_s = placed([P, 30 * KIB // 4], I32, "tab_s", AT_TABLE_SCALES)[:, 0 : T // 4]
        w1_c = [tile([P, PACK, P], U16, f"w1_c{a}") for a in range(PASSES)]
        w1_s = [tile([P, PACK, P], U8, "w1_s0"), placed([P, PACK, P], U8, "w1_s1", AT_W1_PLANE1)]
        v_s = tile([P, S], U8, "v_s")
        v_s1 = tile([P, S // 4], I32, "v_s1")
        vec_rows = tile([P, P], F32, "vec_rows")
        ident = tile([P, P], F32, "ident")
        vec_cols = tile([P, NT], F32, "vec_cols")

        zeros_first = placed([P, P], F32, "zeros_first", AT_TABLE0)
        zeros_second = placed([P, 15 * KIB // 4], I32, "zeros_second", AT_ZEROS_SECOND)[:, 0 : KIB // 4]
        scale_stage = placed([P, PASSES * H // 4], I32, "scale_stage", AT_W1_SCALES)
        w1s_raw = scale_stage[:].rearrange("p (a c) -> p a c", a=PASSES)

        nc.vector.memset(tab_s, 0)
        nc.vector.memset(zeros_first[:], 0.0)
        nc.vector.tensor_copy(vec_rows[:], zeros_first[:])
        nc.vector.memset(zeros_second, 0)
        nc.vector.tensor_copy(scale_stage[:], zeros_second)
        nc.vector.memset(v_s1[:], 0)
        wr_s = tile([P, PASSES, N // 4], I32, "wr_s")
        nc.vector.memset(wr_s[:], 0)
        make_identity(nc, ident[:])

        nc.sync.dma_start(offsets[:], offs)
        tab_s_rows = tab_scales.bitcast(I32).rearrange("a (q r) c -> r q a c", r=PLANE_ROWS)
        for r in range(PLANE_ROWS):
            nc.sync.dma_start(tab_s[r:P:PASS_ROWS, :], tab_s_rows[r])
        bias = tile([P, PACK], F32, "bias")
        nc.sync.dma_start(bias[:], b1.rearrange("(p t) -> p t", t=PACK))
        nc.sync.dma_start(vec_rows[0:NT, :], gr.rearrange("(c p) -> c p", p=P))
        tab_w_rows = tab_words.rearrange("a p t i -> a p (t i)").bitcast(I32)
        tab_w = [placed([P, T], I32, "tab_w0", AT_TABLE0), placed([P, T], I32, "tab_w1", AT_TABLE1)]
        nc.sync.dma_start(tab_w[0][:], tab_w_rows[0])
        w1s_rows = w1_scales.bitcast(I32).rearrange("a q c -> q a c")
        for q in range(QUADS):
            nc.sync.dma_start(
                w1s_raw[32 * q : 32 * q + PLANE_ROWS, :, :], w1s_rows[PLANE_ROWS * q : PLANE_ROWS * (q + 1)]
            )
        w1_raw = [placed([P, H // 2], I32, f"w1_raw{a}", AT_W1[a]) for a in range(PASSES)]
        nc.sync.dma_start(w1_raw[0][:], w1_words.bitcast(I32)[0])
        nc.sync.dma_start(tab_w[1][:], tab_w_rows[1])
        nc.sync.dma_start(w1_raw[1][:], w1_words.bitcast(I32)[1])
        wrs_rows = wr_scales.bitcast(I32).rearrange("a q c -> q a c")
        for q in range(QUADS):
            nc.sync.dma_start(
                wr_s[32 * q : 32 * q + PLANE_ROWS, :, :], wrs_rows[PLANE_ROWS * q : PLANE_ROWS * (q + 1)]
            )
        wl_rows = wl.rearrange("(a p i) n -> a p i n", a=PASSES, i=PACK)

        banks = [psum.tile([P, JW], F32, name=f"bank{b}") for b in range(BANKS)]
        nc.tensor.transpose(banks[-1][:, 0:P], vec_rows[:], ident[:])
        nc.scalar.copy(vec_cols[:], banks[-1][:, 0:NT])

        nc.vector.tensor_copy(v_s[:], tab_s.bitcast(U8).indirect(offsets[:]))
        nc.sync.dma_start(v_s1[0:SHIFT_ROWS, :], v_s[PASS_ROWS:P, :].bitcast(I32))
        for a, copy in enumerate((nc.vector.tensor_copy, nc.gpsimd.tensor_copy)):
            nc.scalar.copy(w1_c[a][:], w1_raw[a][:].bitcast(U16).rearrange("p (m t) -> p t m", t=PACK))
            copy(w1_s[a][:], w1s_raw[:, a, :].bitcast(U8).rearrange("p (m t) -> p t m", t=PACK))

        w2_raw = placed([P, PACK, N], F32, "w2_raw", AT_W2)
        wl_next = placed([P, PACK, NH], F32, "wl_next", AT_WL_NEXT)
        wl_late = [placed([P, PACK, NH], F32, f"wl_late{u}", AT_WL_LATE + 4 * KIB * u) for u in range(2)]
        wl_early = placed([P, PACK, NH], F32, "wl_early", AT_WL_EARLY)
        nc.sync.dma_start(wl_early[:], wl_rows[0][:, :, 0:NH])
        wr_c = placed([P, PASSES, N], I32, "wr_c", AT_WR)
        nc.sync.dma_start(
            wr_c[:], wr_words.rearrange("a p c i -> a p (c i)").bitcast(I32).rearrange("a p c -> p a c")
        )
        nc.sync.dma_start(wl_next[:], wl_rows[1][:, :, 0:NH])
        nc.sync.dma_start(w2_raw[:], w2.rearrange("(p t) n -> p t n", t=PACK))
        for a in range(PASSES):
            nc.sync.dma_start(wl_late[a][:], wl_rows[a][:, :, NH:N])

        v_c = [
            [tile([P, JW], U32, "v_c00"), placed([P, JW], U32, "v_c01", AT_V01)],
            [tile([P, JW], U32, "v_c10"), tile([P, JW], U32, "v_c11")],
        ]

        def gather_words(a, jb, first, width):
            column = (jb * JW + first) // 16
            nc.vector.tensor_copy(
                v_c[a][jb][:, first : first + width],
                tab_w[a][:].bitcast(U32).indirect(offsets[:, column : column + width // 16]),
            )

        gather_words(0, 0, 0, JW)
        gather_words(0, 1, 0, JW)
        gather_words(1, 0, 0, HALF)
        gather_words(1, 0, HALF, HALF)
        gather_words(1, 1, 0, JW)

        def v_plane(a, jb):
            return (v_s[:], v_s1[:].bitcast(U8))[a][:, jb * JW : (jb + 1) * JW]

        for n in range(WARM_UP):
            nc.tensor.matmul_mx(
                out=banks[0][:],
                lhsT=tab_w[0][:, 0:P].bitcast(FP8X4),
                lhsT_scale=v_s[:, 0:P],
                rhs=tab_w[0][:, 0:JW].bitcast(FP8X4),
                rhs_scale=v_s[:, 0:JW],
                start=True,
                stop=True,
            )

        def interleave(copy, dst, src):
            copy(
                dst.rearrange("p (c i t) -> p c t i", i=4, t=PACK),
                src.rearrange("p t (c i) -> p c t i", i=4),
            )

        def grouped(copy, src, name, at=None):
            shape = [P, PACK * src.shape[2]]
            dst = tile(shape, BF16, name) if at is None else placed(shape, BF16, name, at)
            interleave(copy, dst[:], src)
            return dst

        def quantize(values, name, at=None):
            width = values.shape[1] // PACK
            codes = tile([P, width], U32, name + "_c") if at is None else placed([P, width], U32, name + "_c", at)
            scales = tile([P, width], U8, name + "_s")
            nc.vector.quantize_mx(out=codes[:].bitcast(FP8X4), scales=scales[:], in_=values[:])
            return codes, scales

        h_rows = [tile([P, PACK, JW], BF16, f"h_rows{jb}") for jb in range(JB)]

        def hidden_pass(acc, t, jb, a, first, width, start, stop):
            nc.tensor.matmul_mx(
                out=acc,
                lhsT=w1_c[a][:, t, :].bitcast(U8).bitcast(FP4X4),
                lhsT_scale=w1_s[a][:, t, :],
                rhs=v_c[a][jb][:, first : first + width].bitcast(FP8X4),
                rhs_scale=v_plane(a, jb)[:, first : first + width],
                start=start,
                stop=stop,
            )

        def relu(acc, t, jb, first, width, by_vector):
            dst = h_rows[jb][:, t, first : first + width]
            if by_vector:
                nc.vector.tensor_scalar(dst, acc, bias[:, t : t + 1], 0.0, ALU.add, ALU.max)
            else:
                nc.scalar.activation(dst, acc, ACT.Relu, bias=bias[:, t : t + 1])

        first_banks = [banks[5], banks[6], banks[7], banks[0]]

        def second_sum(t):
            return banks[2 + t // 2][:, (t % 2) * HALF : (t % 2 + 1) * HALF]

        for t in range(PACK):
            hidden_pass(first_banks[t][:, 0:HALF], t, 0, 0, 0, HALF, True, False)
        for t in range(PACK):
            hidden_pass(second_sum(t), t, 0, 0, HALF, HALF, t % 2 == 0, False)
        hidden_pass(banks[PACK][:], 0, 1, 0, 0, JW, True, False)
        for t in range(PACK):
            hidden_pass(first_banks[t][:, 0:HALF], t, 0, 1, 0, HALF, False, True)
            relu(first_banks[t][:, 0:HALF], t, 0, 0, HALF, False)
        for pair in range(2):
            for t in (2 * pair, 2 * pair + 1):
                hidden_pass(second_sum(t), t, 0, 1, HALF, HALF, False, t % 2 == 1)
            for t in (2 * pair, 2 * pair + 1):
                relu(second_sum(t), t, 0, HALF, HALF, pair == 1)
        for t in (1, 2):
            hidden_pass(banks[PACK + t][:], t, 1, 0, 0, JW, True, False)
        for t in range(PACK):
            if t == PACK - 1:
                hidden_pass(banks[PACK + t][:], t, 1, 0, 0, JW, True, False)
            hidden_pass(banks[PACK + t][:], t, 1, 1, 0, JW, False, True)
            relu(banks[PACK + t][:], t, 1, 0, JW, False)

        refs, h_q, wl_q = {}, {}, {}

        def reference_tile(c, jb):
            acc = banks[NT * jb + c]
            for a in range(PASSES):
                nc.tensor.matmul_mx(
                    out=acc[:],
                    lhsT=wr_c[:, a, c * P : (c + 1) * P].bitcast(FP8X4),
                    lhsT_scale=wr_s[:, a, :].bitcast(U8)[:, c * P : (c + 1) * P],
                    rhs=v_c[a][jb][:].bitcast(FP8X4),
                    rhs_scale=v_plane(a, jb),
                    start=(a == 0),
                    stop=(a == PASSES - 1),
                )
            if (c, jb) == (0, 0):
                ref = placed([P, JW], F32, "ref00", AT_FIRST_REF)[:]
            else:
                ref = tile([P, JW], F32, f"ref{c}{jb}")[:]
            gain = vec_cols[:, c : c + 1]
            if (c, jb) == (NT - 1, JB - 1):
                nc.vector.tensor_scalar(ref, acc[:], gain, None, ALU.mult)
            else:
                nc.scalar.activation(ref, acc[:], ACT.Copy, scale=gain)
            refs[(c, jb)] = ref

        def estimate_sum(c, jb, cols):
            if (c, jb) == (NT - 1, JB - 1) and cols.start >= HALF:
                return banks[0][:, cols]
            return banks[NT * jb + c][:, cols]

        def estimate_pass(c, jb, cols, stationary, first, moving, moving_scales, start, stop):
            codes, scales = stationary
            nc.tensor.matmul_mx(
                out=estimate_sum(c, jb, cols),
                lhsT=codes[:, first : first + P].bitcast(FP8X4),
                lhsT_scale=scales[:, first : first + P],
                rhs=moving[:, cols].bitcast(FP8X4),
                rhs_scale=moving_scales[:, cols],
                start=start,
                stop=stop,
            )

        def linear_passes(c, jb, opens, cols=slice(0, JW)):
            for a in range(PASSES):
                first = a * NH + (c % 2) * P
                start, stop = opens and a == 0, not opens and a == PASSES - 1
                estimate_pass(c, jb, cols, wl_q[c // 2], first, v_c[a][jb][:], v_plane(a, jb), start, stop)

        def branch_pass(c, jb, opens, cols=slice(0, JW)):
            estimate_pass(c, jb, cols, w2_q, c * P, h_q[jb][0][:], h_q[jb][1][:], opens, not opens)

        def finish_tile(c, jb, widths=(JW,)):
            diff = tile([P, JW], F32, f"diff{c}{jb}")
            err = tile([P, JW], F32, f"err{c}{jb}")
            for piece, width in enumerate(widths):
                cols = slice(sum(widths[:piece]), sum(widths[:piece]) + width)
                nc.vector.tensor_tensor(diff[:, cols], estimate_sum(c, jb, cols), refs[(c, jb)][:, cols], ALU.subtract)
                nc.scalar.activation(err[:, cols], diff[:, cols], ACT.Abs)
                nc.sync.dma_start(out[c * P : (c + 1) * P, jb * JW : (jb + 1) * JW][:, cols], err[:, cols])

        on_vector, on_scalar = nc.vector.tensor_copy, nc.scalar.copy

        wl_first = tile([P, PACK * N], BF16, "wl_first")
        nc.gpsimd.tensor_scalar(
            wl_first[:, 0 : PACK * NH].rearrange("p (c t) -> p c t", t=PACK),
            wl_early[:].rearrange("p t c -> p c t"),
            1.0,
            0.0,
            ALU.mult,
            ALU.add,
        )
        h_first = tile([P, PACK * JW], BF16, "h_first")
        for half in range(2):
            interleave(
                on_vector,
                h_first[:, half * PACK * HALF : (half + 1) * PACK * HALF],
                h_rows[0][:, :, half * HALF : (half + 1) * HALF],
            )
        interleave(on_vector, wl_first[:, PACK * NH : PACK * N], wl_next[:])
        h_q[0] = quantize(h_first, "h_first")
        wl_q[0] = quantize(wl_first, "wl_first")
        h_second = grouped(on_vector, h_rows[1][:], "h_second")
        w2_grouped = grouped(on_vector, w2_raw[:], "w2_grouped")
        h_q[1] = quantize(h_second, "h_second")
        w2_q = quantize(w2_grouped, "w2")
        for c in range(NT):
            reference_tile(c, 0)
        for c in (0, 1):
            reference_tile(c, 1)
        wl_second = tile([P, PACK * N], BF16, "wl_second")
        interleave(on_scalar, wl_second[:, 0 : PACK * NH], wl_late[0][:])
        split = NH - LAST_ON_VECTOR
        interleave(on_scalar, wl_second[:, PACK * NH : PACK * (NH + split)], wl_late[1][:, :, 0:split])
        for c in (2, 3):
            reference_tile(c, 1)
        interleave(on_vector, wl_second[:, PACK * (NH + split) :], wl_late[1][:, :, split:NH])
        linear_passes(0, 0, True)
        linear_passes(1, 0, True)
        branch_pass(0, 0, False)
        branch_pass(1, 0, False)
        for c in (0, 1):
            linear_passes(c, 1, True)
            branch_pass(c, 1, False)
        finish_tile(0, 0)
        wl_q[1] = quantize(wl_second, "wl_second", AT_FIRST_REF)
        finish_tile(1, 0)
        finish_tile(0, 1)
        finish_tile(1, 1)
        for jb in range(JB):
            for c in (2, 3):
                last = (c, jb) == (NT - 1, JB - 1)
                for cols in (slice(0, HALF), slice(HALF, JW)) if last else (slice(0, JW),):
                    branch_pass(c, jb, True, cols)
                    linear_passes(c, jb, False, cols)
                finish_tile(c, jb, ((JW,), (JW,), (HALF, HALF), (HALF, P, P))[2 * jb + c - 2])
